import numpy as np
import ml_dtypes


def mxq(x, axis, fmt="e4m3"):
    dtype, down = {"e4m3": (ml_dtypes.float8_e4m3fn, 7), "e5m2": (ml_dtypes.float8_e5m2, 14)}[fmt]
    v = np.moveaxis(np.asarray(x, np.float32).astype(ml_dtypes.bfloat16).astype(np.float64), axis, -1)
    blocks = v.reshape(v.shape[:-1] + (-1, 32))
    amax = np.abs(blocks).max(-1, keepdims=True)
    byte = np.maximum(np.where(amax > 0, np.frexp(amax)[1] - 1 + 127, 0) - down, 1)
    scale = np.exp2(byte - 127.0)
    codes = (blocks / scale).astype(np.float32).astype(dtype).astype(np.float64)
    return np.moveaxis((codes * scale).reshape(v.shape), -1, axis)


WIDE = False


def mx_kscale(k):
    if not WIDE:
        return np.ones(k)
    levels = np.array([10, -10, 5, -5, 0])
    if k % 512:
        return np.exp2(np.random.permutation(np.resize(levels, k // 32))).repeat(32)
    a = np.empty((k // 512, 16))
    for p in range(k // 512):
        a[p, :8] = np.random.permutation(np.resize(levels, 8))
        for g in range(8):
            far = levels[np.abs(levels - a[p, g]) >= 10]
            a[p, g + 8] = far[np.random.randint(len(far))]
    return np.exp2(a.ravel()).repeat(32)


def f64(x):
    return np.asarray(x).astype(np.float64)


def striped(idx):
    return np.tile(idx.reshape(-1, 16).T, (8, 1)).astype(np.uint16)


def unstriped(offs):
    return offs[:16].T.reshape(-1).astype(np.int64)


E2M1 = np.array([0.0, 0.5, 1.0, 1.5, 2.0, 3.0, 4.0, 6.0, -0.0, -0.5, -1.0, -1.5, -2.0, -3.0, -4.0, -6.0])


def pack_weight(w, fmt):
    k, n = w.shape
    w = f64(np.asarray(w, np.float32).astype(ml_dtypes.bfloat16)).reshape(k // 32, 32, n)
    amax = np.abs(w).max(1)
    if fmt == "e4m3":
        byte = np.frexp(amax)[1] - 1 + 127 - 7
    else:
        mant, ex = np.frexp(amax / 6.0)
        byte = np.where(mant > 0.5, ex, ex - 1) + 127
    byte = np.clip(np.where(amax > 0, byte, 1), 1, 254)
    scaled = (w * np.exp2(127.0 - byte)[:, None, :]).reshape(k, n).astype(np.float32)
    by_word = np.ascontiguousarray(scaled.reshape(k // 512, 128, 4, n).transpose(0, 1, 3, 2))
    if fmt == "e4m3":
        words = by_word.astype(ml_dtypes.float8_e4m3fn).view(np.uint8)
    else:
        c = by_word.astype(ml_dtypes.float4_e2m1fn).view(np.uint8) & 0xF
        words = (c[..., 0::2] | (c[..., 1::2] << 4)).reshape(k // 512, 128, 2 * n)
    return np.ascontiguousarray(words), np.ascontiguousarray(byte.astype(np.uint8).reshape(k // 512, 16, n))


def unpack_weight(words, scales, fmt):
    g, _, n = scales.shape
    words = np.ascontiguousarray(words).reshape(g, 128, n, -1)
    if fmt == "e4m3":
        vals = words.view(ml_dtypes.float8_e4m3fn).astype(np.float64)
    else:
        nib = np.empty((g, 128, n, 4), np.uint8)
        nib[..., 0::2] = words & 0xF
        nib[..., 1::2] = words >> 4
        vals = E2M1[nib]
    vals = vals * np.repeat(np.exp2(scales.astype(np.float64) - 127.0), 8, axis=1)[..., None]
    return vals.transpose(0, 1, 3, 2).reshape(g * 512, n)


def gelu(v):
    return 0.5 * v * (1.0 + np.tanh(np.sqrt(2.0 / np.pi) * (v + 0.044715 * v**3)))


K, H, N, T, S, T2, P = 1024, 1024, 512, 4096, 1024, 2048, 1024

def setup_inputs():
    n = np.random.standard_normal
    s = mx_kscale(K)[:, None]
    u = mx_kscale(H)[:, None]
    tab_words, tab_scales = pack_weight(n((K, T)) * s, "e4m3")
    w4_words, w4_scales = pack_weight(n((K, H)) / np.sqrt(K) / s, "e2m1")
    w8_words, w8_scales = pack_weight(n((H, N)) / np.sqrt(H) / u, "e4m3")
    return {
        "tab_words": tab_words, "tab_scales": tab_scales,
        "offs": striped(np.random.permutation(T)[:S]),
        "offs2": striped(np.random.permutation(T2)[:S]),
        "offs3": striped(np.random.permutation(T2)[:P]),
        "offs4": striped(np.random.permutation(T2)[:P]),
        "w4_words": w4_words, "w4_scales": w4_scales,
        "bg": (0.5 * n(H)).astype(np.float32),
        "wv": (n((K, H)) / np.sqrt(K) / s * u.T).astype(np.float32),
        "wgs": np.exp(0.3 * n((128, S))).astype(np.float32),
        "page0": (0.7 * n((H, T2)) * u).astype(np.float32),
        "w8_words": w8_words, "w8_scales": w8_scales,
    }

def reference(tab_words, tab_scales, offs, offs2, offs3, offs4, w4_words, w4_scales,
              bg, wv, wgs, page0, w8_words, w8_scales):
    v = unpack_weight(tab_words, tab_scales, "e4m3")[:, unstriped(offs)]
    a = (unpack_weight(w4_words, w4_scales, "e2m1").T @ v) + f64(bg)[:, None]
    b = mxq(f64(wv), 0, "e4m3").T @ v
    h = b / (1 + np.exp(-a))
    page = f64(page0).copy()
    page[:, unstriped(offs2)] = np.tile(f64(wgs), (H // 128, 1)) * h
    x1 = page[:, unstriped(offs3)]
    x2 = page[:, unstriped(offs4)]
    z = np.maximum(x1, x2)
    return unpack_weight(w8_words, w8_scales, "e4m3").T @ mxq(z, 0, "e4m3")

@@ -1,0 +1,332 @@
+from contextlib import ExitStack
+
+import concourse.mybir as mybir
+from concourse.masks import make_identity
+
+K, H, N, T, S, T2, M = 1024, 1024, 512, 4096, 1024, 2048, 1024
+FLOPS = 2 * (2 * K * H * S + H * N * M)
+
+F32 = mybir.dt.float32
+BF16 = mybir.dt.bfloat16
+I32 = mybir.dt.int32
+U32 = mybir.dt.uint32
+U16 = mybir.dt.uint16
+U8 = mybir.dt.uint8
+FP8X4 = mybir.dt.float8_e4m3fn_x4
+FP4X4 = mybir.dt.float4_e2m1fn_x4
+MULT = mybir.AluOpType.mult
+MAX = mybir.AluOpType.max
+SIGMOID = mybir.ActivationFunctionType.Sigmoid
+
+P = 128
+PACK = 4
+PASSES = 2
+BANK = 512
+ROW_TILES = H // P
+TILES_PER_PASS = ROW_TILES // PASSES
+WIDTHS = [256, 256, 256, 128, 128]
+STARTS = [sum(WIDTHS[:c]) for c in range(len(WIDTHS))]
+CHUNKS = len(WIDTHS)
+N_TILES = N // P
+LIST = 16
+W4_HEAD = 2
+AHEAD = 3
+
+
+def tile_list_merge_conflict_scores_kernel(
+    tc, tab_words, tab_scales, offs, offs2, offs3, offs4, w4_words, w4_scales,
+    bg, wv, wgs, page0, w8_words, w8_scales, out,
+):
+    nc = tc.nc
+    with ExitStack() as ctx:
+        lists = ctx.enter_context(tc.tile_pool(name="lists", bufs=1))
+        keep = ctx.enter_context(tc.tile_pool(name="keep", bufs=1))
+        ring = ctx.enter_context(tc.tile_pool(name="ring", bufs=2))
+        psum = ctx.enter_context(tc.psum_pool(name="psum", bufs=2))
+
+        def load_list(src, name):
+            tile = lists.tile([P, S // LIST], U16, name=name)
+            nc.sync.dma_start(tile[:], src)
+            return tile
+
+        def entries(tile, first, count):
+            return tile[:, first // LIST : (first + count) // LIST]
+
+        def zero_plane(engine, plane):
+            engine.memset(plane[:].rearrange("p a c -> p (a c)").bitcast(I32), 0)
+
+        def load_plane(queue, plane, scales):
+            for q in range(4):
+                queue.dma_start(
+                    plane[:].bitcast(I32)[32 * q : 32 * q + 4, :, :],
+                    scales.bitcast(I32)[:, 4 * q : 4 * q + 4, :].rearrange("a r c -> r a c"),
+                )
+
+        tab_plane = keep.tile([P, PASSES, T], U8, align_bytes=64)
+        zero_plane(nc.vector, tab_plane)
+        bg_rows = keep.tile([P, P], F32)
+        nc.vector.memset(bg_rows[:], 0.0)
+        warm = keep.tile([P, 1], F32)
+        nc.scalar.activation(warm[:], bg_rows[:, P - 1 : P], SIGMOID)
+        w4_plane = keep.tile([P, PASSES, H], U8, align_bytes=64)
+        zero_plane(nc.gpsimd, w4_plane)
+        load_plane(nc.gpsimd, w4_plane, w4_scales)
+        ident_f32 = keep.tile([P, P], F32)
+        make_identity(nc, ident_f32[:])
+        ident_bf16 = keep.tile([P, P], BF16)
+        make_identity(nc, ident_bf16[:])
+        w8_plane = keep.tile([P, PASSES, N], U8, align_bytes=64)
+        zero_plane(nc.gpsimd, w8_plane)
+
+        tab = [keep.tile([P, T], I32, name="tab%d" % a) for a in range(PASSES)]
+        tab_src = [tab_words[a].rearrange("p t i -> p (t i)").bitcast(I32) for a in range(PASSES)]
+        nc.sync.dma_start(tab[0][:, : T // 4], tab_src[0][:, : T // 4])
+        load_plane(nc.sync, tab_plane, tab_scales)
+        idx = load_list(offs, "idx")
+        nc.sync.dma_start(tab[0][:, T // 4 :], tab_src[0][:, T // 4 :])
+        nc.sync.dma_start(tab[1][:, : T // 2], tab_src[1][:, : T // 2])
+        nc.sync.dma_start(bg_rows[0:ROW_TILES, :], bg.rearrange("(i p) -> i p", p=P))
+
+        w4_src = w4_words.bitcast(I32).rearrange("a p c -> p a c")
+        head_words = W4_HEAD * P // 2
+        w4_head = keep.tile([P, PASSES, 4 * head_words], U8, align_bytes=64)
+        nc.sync.dma_start(w4_head[:].bitcast(I32), w4_src[:, :, 0:head_words])
+        w4_rest = keep.tile([P, PASSES, 2 * H - 4 * head_words], U8, align_bytes=64)
+
+        def w4_codes(a, i):
+            if i < W4_HEAD:
+                return w4_head[:, a, 2 * P * i : 2 * P * (i + 1)]
+            return w4_rest[:, a, 2 * P * (i - W4_HEAD) : 2 * P * (i - W4_HEAD + 1)]
+
+        wv_raw, pages = {}, {}
+
+        def load_wv(i):
+            raw = ring.tile([P, PASSES, PACK, P], F32, name="wv_raw", bufs=3)
+            for a in range(PASSES):
+                rows = wv[a * P * PACK : (a + 1) * P * PACK, i * P : (i + 1) * P]
+                nc.sync.dma_start(raw[:, a, :, :], rows.rearrange("(p j) c -> p j c", j=PACK))
+            wv_raw[i] = raw
+
+        def load_page(i):
+            page = ring.tile([P, T2], F32, name="page", bufs=4)
+            nc.sync.dma_start(page[:], page0[i * P : (i + 1) * P, :])
+            pages[i] = page
+
+        load_wv(0)
+        nc.sync.dma_start(tab[1][:, T // 2 :], tab_src[1][:, T // 2 :])
+        gains = keep.tile([P, S], F32)
+        nc.sync.dma_start(gains[:], wgs)
+        load_page(0)
+        idx2 = load_list(offs2, "idx2")
+        load_wv(1)
+        load_wv(2)
+        idx3 = load_list(offs3, "idx3")
+        idx4 = load_list(offs4, "idx4")
+        nc.sync.dma_start(w4_rest[:].bitcast(I32), w4_src[:, :, head_words:])
+
+        bg_turned = psum.tile([P, P], F32, name="turn2")
+        nc.tensor.transpose(bg_turned[:], bg_rows[:], ident_f32[:])
+        bias = keep.tile([P, ROW_TILES], F32)
+        nc.scalar.copy(bias[:], bg_turned[:, 0:ROW_TILES])
+
+        v_codes = [keep.tile([P, S], U32, name="v_codes%d" % a, align_bytes=64) for a in range(PASSES)]
+        v_plane = [keep.tile([P, S], U8, name="v_plane%d" % a, align_bytes=64) for a in range(PASSES)]
+        for a in range(PASSES):
+            nc.vector.tensor_copy(v_plane[a][:], tab_plane[:, a, :].indirect(idx[:]))
+        nc.vector.tensor_copy(v_codes[0][:], tab[0][:].bitcast(U32).indirect(idx[:]))
+        for h in range(S // BANK):
+            nc.vector.tensor_copy(
+                v_codes[1][:, h * BANK : (h + 1) * BANK],
+                tab[1][:].bitcast(U32).indirect(entries(idx, h * BANK, BANK)),
+            )
+
+        wv_grouped, wv_codes, wv_plane = {}, {}, {}
+
+        def group_wv(i):
+            grouped = ring.tile([P, PASSES, P, PACK], BF16, name="wv_grouped", align_bytes=64)
+            for a in range(PASSES):
+                nc.scalar.copy(
+                    grouped[:, a, :, :].rearrange("p (c e) j -> p c j e", e=4),
+                    wv_raw[i][:, a, :, :].rearrange("p j (c e) -> p c j e", e=4),
+                )
+            wv_grouped[i] = grouped
+
+        def quantize_wv(i):
+            codes = ring.tile([P, PASSES * P], U32, name="wv_codes", bufs=4, align_bytes=64)
+            plane = ring.tile([P, PASSES * P], U8, name="wv_plane", bufs=4, align_bytes=64)
+            nc.vector.quantize_mx(
+                out=codes[:].bitcast(FP8X4),
+                scales=plane[:],
+                in_=wv_grouped[i][:].rearrange("p a c j -> p (a c j)"),
+            )
+            wv_codes[i], wv_plane[i] = codes, plane
+
+        gates, values = {}, {}
+
+        def products(i):
+            sig = ring.tile([P, S], F32, name="sig")
+            gate = ring.tile([P, S], F32, name="gate")
+            value = ring.tile([P, S], F32, name="value", align_bytes=64)
+            halves = [slice(h * BANK, (h + 1) * BANK) for h in range(S // BANK)]
+            pre = [psum.tile([P, BANK], F32, name="pre", tag="acc", bufs=4) for h in halves]
+            lin = [psum.tile([P, BANK], F32, name="lin", tag="acc", bufs=4) for h in halves]
+            for a in range(PASSES):
+                for h, cols in enumerate(halves):
+                    for acc, codes, plane in (
+                        (pre[h], w4_codes(a, i).bitcast(FP4X4), w4_plane[:, a, i * P : (i + 1) * P]),
+                        (lin[h], wv_codes[i][:, a * P : (a + 1) * P].bitcast(FP8X4), wv_plane[i][:, a * P : (a + 1) * P]),
+                    ):
+                        nc.tensor.matmul_mx(
+                            out=acc[:],
+                            lhsT=codes,
+                            lhsT_scale=plane,
+                            rhs=v_codes[a][:, cols].bitcast(FP8X4),
+                            rhs_scale=v_plane[a][:, cols],
+                            start=(a == 0),
+                            stop=(a == PASSES - 1),
+                        )
+            gate_engine = nc.vector if i == 0 else nc.gpsimd
+            for h, cols in enumerate(halves):
+                nc.scalar.activation(sig[:, cols], pre[h][:], SIGMOID, bias=bias[:, i : i + 1])
+                gate_engine.tensor_tensor(gate[:, cols], sig[:, cols], gains[:, cols], MULT)
+                nc.scalar.copy(value[:, cols], lin[h][:])
+            gates[i], values[i] = gate, value
+
+        def scatter(i):
+            nc.vector.tensor_tensor(pages[i][:].indirect(idx2[:]), values[i][:], gates[i][:], MULT)
+
+        def fetch(dst, i, lst, first, count):
+            nc.vector.tensor_copy(dst, pages[i][:].indirect(entries(lst, first, count)))
+
+        z_rows = [
+            [keep.tile([P, w // P, P * PACK], BF16, name="z_rows%d_%d" % (a, c)) for c, w in enumerate(WIDTHS)]
+            for a in range(PASSES)
+        ]
+
+        def turn_first(i, c, z):
+            a, slot = divmod(i, TILES_PER_PASS)
+            blocks = WIDTHS[c] // P
+            turned = psum.tile([P, blocks, P], BF16, name="turn1")
+            for b in range(blocks):
+                nc.tensor.transpose(turned[:, b, :], z[:, b * P : (b + 1) * P], ident_bf16[:])
+            nc.scalar.copy(z_rows[a][c][:, :, slot * P : (slot + 1) * P], turned[:])
+
+        def turn_second(a, c, grouped):
+            blocks = WIDTHS[c] // P
+            words = z_rows[a][c][:].bitcast(F32)
+            turned = psum.tile([P, blocks, 2, P], F32, name="turn2")
+            for b in range(blocks):
+                for u in range(2):
+                    nc.tensor.transpose(turned[:, b, u, :], words[:, b, u : 2 * P : 2], ident_f32[:])
+            nc.scalar.copy(
+                grouped.bitcast(F32).rearrange("p (b m u) -> p b m u", b=blocks, u=2),
+                turned[:].rearrange("p b u m -> p b m u"),
+            )
+
+        z_codes = [keep.tile([P, M], U32, name="z_codes%d" % a, align_bytes=64) for a in range(PASSES)]
+        z_plane = [keep.tile([P, M], U8, name="z_plane%d" % a, align_bytes=64) for a in range(PASSES)]
+
+        def chunk(c):
+            return slice(STARTS[c], STARTS[c] + WIDTHS[c])
+
+        def quantize_z(a, cols, grouped):
+            nc.vector.quantize_mx(out=z_codes[a][:, cols].bitcast(FP8X4), scales=z_plane[a][:, cols], in_=grouped)
+
+        w8_codes = keep.tile([P, PASSES, N], I32, align_bytes=64)
+        sums = {}
+
+        def score_pass(a, c):
+            for pair in range(N_TILES // 2):
+                if a == 0:
+                    sums[c, pair] = psum.tile([P, 2, WIDTHS[c]], F32, name="score", tag="acc", bufs=4)
+                for e in range(2):
+                    t = 2 * pair + e
+                    nc.tensor.matmul_mx(
+                        out=sums[c, pair][:, e, :],
+                        lhsT=w8_codes[:, a, t * P : (t + 1) * P].bitcast(FP8X4),
+                        lhsT_scale=w8_plane[:, a, t * P : (t + 1) * P],
+                        rhs=z_codes[a][:, chunk(c)].bitcast(FP8X4),
+                        rhs_scale=z_plane[a][:, chunk(c)],
+                        start=(a == 0 and e == 0),
+                        stop=(a == PASSES - 1 and e == 1),
+                    )
+
+        out_tiles = out.rearrange("(t p) m -> p t m", p=P)
+
+        def store_scores(c):
+            for pair in range(N_TILES // 2):
+                staged = ring.tile([P, 2, WIDTHS[c]], F32, name="staged", bufs=4)
+                if c == CHUNKS - 1 and pair == 1:
+                    nc.vector.tensor_copy(staged[:], sums[c, pair][:])
+                else:
+                    nc.scalar.copy(staged[:], sums[c, pair][:])
+                nc.sync.dma_start(out_tiles[:, 2 * pair : 2 * pair + 2, chunk(c)], staged[:])
+
+        group_wv(0)
+        quantize_wv(0)
+        products(0)
+        for i in range(1, AHEAD):
+            group_wv(i)
+            quantize_wv(i)
+        last = ROW_TILES - 1
+        ours = {}
+        first_pass = keep.tile([P, M * PACK], BF16, align_bytes=64)
+        for i in range(ROW_TILES):
+            if i + AHEAD < ROW_TILES:
+                load_wv(i + AHEAD)
+            if i < last:
+                load_page(i + 1)
+                products(i + 1)
+            if i == 1:
+                nc.sync.dma_start(w8_codes[:], w8_words.rearrange("a p c i -> p a (c i)").bitcast(I32))
+                load_plane(nc.sync, w8_plane, w8_scales)
+            scatter(i)
+            if i == last:
+                break
+            theirs = values[i][:].bitcast(BF16)[:, 0:M]
+            if i > 0:
+                fetch(theirs, i - 1, idx4, 0, M)
+            ours[i] = ring.tile([P, M], BF16, name="ours")
+            fetch(ours[i][:], i, idx3, 0, M)
+            if i + AHEAD < ROW_TILES:
+                group_wv(i + AHEAD)
+                quantize_wv(i + AHEAD)
+            if i == TILES_PER_PASS + 1:
+                quantize_z(0, slice(0, M), first_pass[:])
+            if i > 0:
+                best = ring.tile([P, M], BF16, name="best")
+                nc.vector.tensor_tensor(best[:], ours[i - 1][:], theirs, MAX)
+                for c in range(CHUNKS):
+                    turn_first(i - 1, c, best[:, chunk(c)])
+            if i == TILES_PER_PASS:
+                for c in range(CHUNKS):
+                    turn_second(0, c, first_pass[:, PACK * STARTS[c] : PACK * (STARTS[c] + WIDTHS[c])])
+
+        widest = max(WIDTHS)
+        stage = [values[last][:].bitcast(BF16)[:, s * PACK * widest : (s + 1) * PACK * widest] for s in range(2)]
+
+        def finish(c):
+            quantize_z(1, chunk(c), stage[c % 2][:, 0 : PACK * WIDTHS[c]])
+            score_pass(1, c)
+            store_scores(c)
+            if c + 2 < CHUNKS:
+                score_pass(0, c + 2)
+
+        score_pass(0, 0)
+        score_pass(0, 1)
+        for c in range(CHUNKS):
+            w = WIDTHS[c]
+            if c >= 2:
+                finish(c - 2)
+            slots = [stage[c % 2][:, s * w : (s + 1) * w] for s in range(3)]
+            fetch(slots[0], last - 1, idx4, STARTS[c], w)
+            fetch(slots[1], last, idx3, STARTS[c], w)
+            fetch(slots[2], last, idx4, STARTS[c], w)
+            best = ring.tile([P, 2, w], BF16, name="best")
+            nc.vector.tensor_tensor(best[:, 0, :], ours[last - 1][:, chunk(c)], slots[0], MAX)
+            nc.vector.tensor_tensor(best[:, 1, :], slots[1], slots[2], MAX)
+            turn_first(last - 1, c, best[:, 0, :])
+            turn_first(last, c, best[:, 1, :])
+            turn_second(1, c, stage[c % 2][:, 0 : PACK * w])
+        finish(CHUNKS - 2)
+        finish(CHUNKS - 1)

@@ -31,6 +31,8 @@ N_TILES = N // P
 LIST = 16
 W4_HEAD = 2
 AHEAD = 3
+EARLY = 2
+SLOTS = 3
 
 
 def tile_list_merge_conflict_scores_kernel(
@@ -62,12 +64,14 @@ def tile_list_merge_conflict_scores_kernel(
                     scales.bitcast(I32)[:, 4 * q : 4 * q + 4, :].rearrange("a r c -> r a c"),
                 )
 
-        tab_plane = keep.tile([P, PASSES, T], U8, align_bytes=64)
-        zero_plane(nc.vector, tab_plane)
+        tab_plane = keep.tile([P, T], U8, align_bytes=64)
+        nc.vector.memset(tab_plane[:].bitcast(I32), 0)
         bg_rows = keep.tile([P, P], F32)
         nc.vector.memset(bg_rows[:], 0.0)
         warm = keep.tile([P, 1], F32)
         nc.scalar.activation(warm[:], bg_rows[:, P - 1 : P], SIGMOID)
+        v_plane = [keep.tile([P, S], U8, name="v_plane%d" % a, align_bytes=64) for a in range(PASSES)]
+        nc.vector.memset(v_plane[1][:].bitcast(I32), 0)
         w4_plane = keep.tile([P, PASSES, H], U8, align_bytes=64)
         zero_plane(nc.gpsimd, w4_plane)
         load_plane(nc.gpsimd, w4_plane, w4_scales)
@@ -81,7 +85,11 @@ def tile_list_merge_conflict_scores_kernel(
         tab = [keep.tile([P, T], I32, name="tab%d" % a) for a in range(PASSES)]
         tab_src = [tab_words[a].rearrange("p t i -> p (t i)").bitcast(I32) for a in range(PASSES)]
         nc.sync.dma_start(tab[0][:, : T // 4], tab_src[0][:, : T // 4])
-        load_plane(nc.sync, tab_plane, tab_scales)
+        for q in range(4):
+            nc.sync.dma_start(
+                tab_plane[:].bitcast(I32)[32 * q : 32 * q + 4 * PASSES, :],
+                tab_scales.bitcast(I32)[:, 4 * q : 4 * q + 4, :],
+            )
         idx = load_list(offs, "idx")
         nc.sync.dma_start(tab[0][:, T // 4 :], tab_src[0][:, T // 4 :])
         nc.sync.dma_start(tab[1][:, : T // 2], tab_src[1][:, : T // 2])
@@ -97,6 +105,12 @@ def tile_list_merge_conflict_scores_kernel(
             if i < W4_HEAD:
                 return w4_head[:, a, 2 * P * i : 2 * P * (i + 1)]
             return w4_rest[:, a, 2 * P * (i - W4_HEAD) : 2 * P * (i - W4_HEAD + 1)]
+
+        def move(engine, dst, src):
+            if engine == "vector":
+                nc.vector.tensor_copy(dst, src)
+            else:
+                nc.scalar.copy(dst, src)
 
         wv_raw, pages = {}, {}
 
@@ -116,9 +130,9 @@ def tile_list_merge_conflict_scores_kernel(
         nc.sync.dma_start(tab[1][:, T // 2 :], tab_src[1][:, T // 2 :])
         gains = keep.tile([P, S], F32)
         nc.sync.dma_start(gains[:], wgs)
+        load_wv(1)
         load_page(0)
         idx2 = load_list(offs2, "idx2")
-        load_wv(1)
         load_wv(2)
         idx3 = load_list(offs3, "idx3")
         idx4 = load_list(offs4, "idx4")
@@ -130,9 +144,12 @@ def tile_list_merge_conflict_scores_kernel(
         nc.scalar.copy(bias[:], bg_turned[:, 0:ROW_TILES])
 
         v_codes = [keep.tile([P, S], U32, name="v_codes%d" % a, align_bytes=64) for a in range(PASSES)]
-        v_plane = [keep.tile([P, S], U8, name="v_plane%d" % a, align_bytes=64) for a in range(PASSES)]
-        for a in range(PASSES):
-            nc.vector.tensor_copy(v_plane[a][:], tab_plane[:, a, :].indirect(idx[:]))
+        nc.vector.tensor_copy(v_plane[0][:], tab_plane[:].indirect(idx[:]))
+        for q in range(4):
+            nc.scalar.dma_start(
+                v_plane[1][:].bitcast(I32)[32 * q : 32 * q + 4, :],
+                v_plane[0][:].bitcast(I32)[32 * q + 4 : 32 * q + 8, :],
+            )
         nc.vector.tensor_copy(v_codes[0][:], tab[0][:].bitcast(U32).indirect(idx[:]))
         for h in range(S // BANK):
             nc.vector.tensor_copy(
@@ -165,30 +182,47 @@ def tile_list_merge_conflict_scores_kernel(
 
         def products(i):
             sig = ring.tile([P, S], F32, name="sig")
-            gate = ring.tile([P, S], F32, name="gate")
             value = ring.tile([P, S], F32, name="value", align_bytes=64)
             halves = [slice(h * BANK, (h + 1) * BANK) for h in range(S // BANK)]
             pre = [psum.tile([P, BANK], F32, name="pre", tag="acc", bufs=4) for h in halves]
             lin = [psum.tile([P, BANK], F32, name="lin", tag="acc", bufs=4) for h in halves]
-            for a in range(PASSES):
+
+            def one_pass(acc, codes, plane, a, cols):
+                nc.tensor.matmul_mx(
+                    out=acc[:],
+                    lhsT=codes,
+                    lhsT_scale=plane,
+                    rhs=v_codes[a][:, cols].bitcast(FP8X4),
+                    rhs_scale=v_plane[a][:, cols],
+                    start=(a == 0),
+                    stop=(a == PASSES - 1),
+                )
+
+            def pre_pass(a, h):
+                one_pass(pre[h], w4_codes(a, i).bitcast(FP4X4), w4_plane[:, a, i * P : (i + 1) * P], a, halves[h])
+
+            def lin_pass(a, h):
+                cols = slice(a * P, (a + 1) * P)
+                one_pass(lin[h], wv_codes[i][:, cols].bitcast(FP8X4), wv_plane[i][:, cols], a, halves[h])
+
+            for h in range(len(halves)):
+                pre_pass(0, h)
+            for h in range(len(halves)):
+                lin_pass(0, h)
+            for h in range(len(halves)):
+                pre_pass(1, h)
+                lin_pass(1, h)
+            if i == 0:
                 for h, cols in enumerate(halves):
-                    for acc, codes, plane in (
-                        (pre[h], w4_codes(a, i).bitcast(FP4X4), w4_plane[:, a, i * P : (i + 1) * P]),
-                        (lin[h], wv_codes[i][:, a * P : (a + 1) * P].bitcast(FP8X4), wv_plane[i][:, a * P : (a + 1) * P]),
-                    ):
-                        nc.tensor.matmul_mx(
-                            out=acc[:],
-                            lhsT=codes,
-                            lhsT_scale=plane,
-                            rhs=v_codes[a][:, cols].bitcast(FP8X4),
-                            rhs_scale=v_plane[a][:, cols],
-                            start=(a == 0),
-                            stop=(a == PASSES - 1),
-                        )
-            gate_engine = nc.vector if i == 0 else nc.gpsimd
+                    nc.scalar.activation(sig[:, cols], pre[h][:], SIGMOID, bias=bias[:, i : i + 1])
+                    nc.vector.tensor_tensor(value[:, cols], lin[h][:], sig[:, cols], MULT)
+                gates[i], values[i] = gains, value
+                return
+            gate = ring.tile([P, S], F32, name="gate", align_bytes=64)
             for h, cols in enumerate(halves):
                 nc.scalar.activation(sig[:, cols], pre[h][:], SIGMOID, bias=bias[:, i : i + 1])
-                gate_engine.tensor_tensor(gate[:, cols], sig[:, cols], gains[:, cols], MULT)
+                nc.gpsimd.tensor_tensor(gate[:, cols], sig[:, cols], gains[:, cols], MULT)
+            for h, cols in enumerate(halves):
                 nc.scalar.copy(value[:, cols], lin[h][:])
             gates[i], values[i] = gate, value
 
@@ -203,22 +237,24 @@ def tile_list_merge_conflict_scores_kernel(
             for a in range(PASSES)
         ]
 
-        def turn_first(i, c, z):
+        def turn_first(i, c, tiles, engine):
             a, slot = divmod(i, TILES_PER_PASS)
             blocks = WIDTHS[c] // P
-            turned = psum.tile([P, blocks, P], BF16, name="turn1")
-            for b in range(blocks):
-                nc.tensor.transpose(turned[:, b, :], z[:, b * P : (b + 1) * P], ident_bf16[:])
-            nc.scalar.copy(z_rows[a][c][:, :, slot * P : (slot + 1) * P], turned[:])
+            turned = psum.tile([P, blocks, len(tiles), P], BF16, name="turn1")
+            for e, z in enumerate(tiles):
+                for b in range(blocks):
+                    nc.tensor.transpose(turned[:, b, e, :], z[:, b * P : (b + 1) * P], ident_bf16[:])
+            move(engine, z_rows[a][c][:, :, slot * P : (slot + len(tiles)) * P], turned[:].rearrange("p b e r -> p b (e r)"))
 
-        def turn_second(a, c, grouped):
+        def turn_second(a, c, grouped, engine):
             blocks = WIDTHS[c] // P
             words = z_rows[a][c][:].bitcast(F32)
             turned = psum.tile([P, blocks, 2, P], F32, name="turn2")
             for b in range(blocks):
                 for u in range(2):
                     nc.tensor.transpose(turned[:, b, u, :], words[:, b, u : 2 * P : 2], ident_f32[:])
-            nc.scalar.copy(
+            move(
+                engine,
                 grouped.bitcast(F32).rearrange("p (b m u) -> p b m u", b=blocks, u=2),
                 turned[:].rearrange("p b u m -> p b m u"),
             )
@@ -255,11 +291,8 @@ def tile_list_merge_conflict_scores_kernel(
 
         def store_scores(c):
             for pair in range(N_TILES // 2):
-                staged = ring.tile([P, 2, WIDTHS[c]], F32, name="staged", bufs=4)
-                if c == CHUNKS - 1 and pair == 1:
-                    nc.vector.tensor_copy(staged[:], sums[c, pair][:])
-                else:
-                    nc.scalar.copy(staged[:], sums[c, pair][:])
+                staged = ring.tile([P, 2, WIDTHS[c]], F32, name="staged", bufs=2 * CHUNKS)
+                move("vector" if c >= EARLY and pair == 1 else "scalar", staged[:], sums[c, pair][:])
                 nc.sync.dma_start(out_tiles[:, 2 * pair : 2 * pair + 2, chunk(c)], staged[:])
 
         group_wv(0)
@@ -297,36 +330,37 @@ def tile_list_merge_conflict_scores_kernel(
                 best = ring.tile([P, M], BF16, name="best")
                 nc.vector.tensor_tensor(best[:], ours[i - 1][:], theirs, MAX)
                 for c in range(CHUNKS):
-                    turn_first(i - 1, c, best[:, chunk(c)])
+                    turn_first(i - 1, c, [best[:, chunk(c)]], "scalar")
             if i == TILES_PER_PASS:
                 for c in range(CHUNKS):
-                    turn_second(0, c, first_pass[:, PACK * STARTS[c] : PACK * (STARTS[c] + WIDTHS[c])])
+                    turn_second(0, c, first_pass[:, PACK * STARTS[c] : PACK * (STARTS[c] + WIDTHS[c])], "scalar")
 
-        widest = max(WIDTHS)
-        stage = [values[last][:].bitcast(BF16)[:, s * PACK * widest : (s + 1) * PACK * widest] for s in range(2)]
+        slot_cols = PACK * max(WIDTHS)
+        spent = [values[last][:].bitcast(BF16), gates[last][:].bitcast(BF16)]
+        stage = [spent[s // 2][:, (s % 2) * slot_cols : (s % 2 + 1) * slot_cols] for s in range(SLOTS)]
 
         def finish(c):
-            quantize_z(1, chunk(c), stage[c % 2][:, 0 : PACK * WIDTHS[c]])
+            if c >= EARLY:
+                score_pass(0, c)
+            quantize_z(1, chunk(c), stage[c % SLOTS][:, 0 : PACK * WIDTHS[c]])
             score_pass(1, c)
             store_scores(c)
-            if c + 2 < CHUNKS:
-                score_pass(0, c + 2)
 
-        score_pass(0, 0)
-        score_pass(0, 1)
+        for c in range(EARLY):
+            score_pass(0, c)
         for c in range(CHUNKS):
             w = WIDTHS[c]
-            if c >= 2:
-                finish(c - 2)
-            slots = [stage[c % 2][:, s * w : (s + 1) * w] for s in range(3)]
+            if c >= SLOTS:
+                finish(c - SLOTS)
+            slots = [stage[c % SLOTS][:, s * w : (s + 1) * w] for s in range(3)]
             fetch(slots[0], last - 1, idx4, STARTS[c], w)
             fetch(slots[1], last, idx3, STARTS[c], w)
             fetch(slots[2], last, idx4, STARTS[c], w)
             best = ring.tile([P, 2, w], BF16, name="best")
             nc.vector.tensor_tensor(best[:, 0, :], ours[last - 1][:, chunk(c)], slots[0], MAX)
             nc.vector.tensor_tensor(best[:, 1, :], slots[1], slots[2], MAX)
-            turn_first(last - 1, c, best[:, 0, :])
-            turn_first(last, c, best[:, 1, :])
-            turn_second(1, c, stage[c % 2][:, 0 : PACK * w])
-        finish(CHUNKS - 2)
-        finish(CHUNKS - 1)
+            engine = "vector" if c == CHUNKS - 1 else "scalar"
+            turn_first(last - 1, c, [best[:, 0, :], best[:, 1, :]], engine)
+            turn_second(1, c, stage[c % SLOTS][:, 0 : PACK * w], engine)
+        for c in range(CHUNKS - SLOTS, CHUNKS):
+            finish(c)

@@ -114,12 +114,15 @@ def tile_list_merge_conflict_scores_kernel(
 
         wv_raw, pages = {}, {}
 
+        def load_wv_pass(i, a):
+            if a == 0:
+                wv_raw[i] = ring.tile([P, PASSES, PACK, P], F32, name="wv_raw", bufs=3)
+            rows = wv[a * P * PACK : (a + 1) * P * PACK, i * P : (i + 1) * P]
+            nc.sync.dma_start(wv_raw[i][:, a, :, :], rows.rearrange("(p j) c -> p j c", j=PACK))
+
         def load_wv(i):
-            raw = ring.tile([P, PASSES, PACK, P], F32, name="wv_raw", bufs=3)
             for a in range(PASSES):
-                rows = wv[a * P * PACK : (a + 1) * P * PACK, i * P : (i + 1) * P]
-                nc.sync.dma_start(raw[:, a, :, :], rows.rearrange("(p j) c -> p j c", j=PACK))
-            wv_raw[i] = raw
+                load_wv_pass(i, a)
 
         def load_page(i):
             page = ring.tile([P, T2], F32, name="page", bufs=4)
@@ -129,11 +132,13 @@ def tile_list_merge_conflict_scores_kernel(
         load_wv(0)
         nc.sync.dma_start(tab[1][:, T // 2 :], tab_src[1][:, T // 2 :])
         gains = keep.tile([P, S], F32)
-        nc.sync.dma_start(gains[:], wgs)
-        load_wv(1)
+        nc.sync.dma_start(gains[:, :BANK], wgs[:, :BANK])
         load_page(0)
         idx2 = load_list(offs2, "idx2")
-        load_wv(2)
+        load_wv(1)
+        load_wv_pass(2, 0)
+        nc.sync.dma_start(gains[:, BANK:], wgs[:, BANK:])
+        load_wv_pass(2, 1)
         idx3 = load_list(offs3, "idx3")
         idx4 = load_list(offs4, "idx4")
         nc.sync.dma_start(w4_rest[:].bitcast(I32), w4_src[:, :, head_words:])
@@ -145,11 +150,7 @@ def tile_list_merge_conflict_scores_kernel(
 
         v_codes = [keep.tile([P, S], U32, name="v_codes%d" % a, align_bytes=64) for a in range(PASSES)]
         nc.vector.tensor_copy(v_plane[0][:], tab_plane[:].indirect(idx[:]))
-        for q in range(4):
-            nc.scalar.dma_start(
-                v_plane[1][:].bitcast(I32)[32 * q : 32 * q + 4, :],
-                v_plane[0][:].bitcast(I32)[32 * q + 4 : 32 * q + 8, :],
-            )
+        nc.scalar.dma_start(v_plane[1][:].bitcast(I32)[0:100, :], v_plane[0][:].bitcast(I32)[4:104, :])
         nc.vector.tensor_copy(v_codes[0][:], tab[0][:].bitcast(U32).indirect(idx[:]))
         for h in range(S // BANK):
             nc.vector.tensor_copy(
@@ -215,8 +216,10 @@ def tile_list_merge_conflict_scores_kernel(
             if i == 0:
                 for h, cols in enumerate(halves):
                     nc.scalar.activation(sig[:, cols], pre[h][:], SIGMOID, bias=bias[:, i : i + 1])
-                    nc.vector.tensor_tensor(value[:, cols], lin[h][:], sig[:, cols], MULT)
-                gates[i], values[i] = gains, value
+                    first, second = (sig, gains) if h == 0 else (gains, sig)
+                    nc.vector.tensor_tensor(value[:, cols], lin[h][:], first[:, cols], MULT)
+                    gates[i, h] = second
+                values[i] = value
                 return
             gate = ring.tile([P, S], F32, name="gate", align_bytes=64)
             for h, cols in enumerate(halves):
@@ -226,8 +229,11 @@ def tile_list_merge_conflict_scores_kernel(
                 nc.scalar.copy(value[:, cols], lin[h][:])
             gates[i], values[i] = gate, value
 
-        def scatter(i):
-            nc.vector.tensor_tensor(pages[i][:].indirect(idx2[:]), values[i][:], gates[i][:], MULT)
+        def scatter(i, gate, first, count):
+            cols = slice(first, first + count)
+            nc.vector.tensor_tensor(
+                pages[i][:].indirect(entries(idx2, first, count)), values[i][:, cols], gate[:, cols], MULT
+            )
 
         def fetch(dst, i, lst, first, count):
             nc.vector.tensor_copy(dst, pages[i][:].indirect(entries(lst, first, count)))
@@ -298,6 +304,7 @@ def tile_list_merge_conflict_scores_kernel(
         group_wv(0)
         quantize_wv(0)
         products(0)
+        scatter(0, gates[0, 0], 0, BANK)
         for i in range(1, AHEAD):
             group_wv(i)
             quantize_wv(i)
@@ -313,7 +320,10 @@ def tile_list_merge_conflict_scores_kernel(
             if i == 1:
                 nc.sync.dma_start(w8_codes[:], w8_words.rearrange("a p c i -> p a (c i)").bitcast(I32))
                 load_plane(nc.sync, w8_plane, w8_scales)
-            scatter(i)
+            if i == 0:
+                scatter(i, gates[0, 1], BANK, BANK)
+            else:
+                scatter(i, gates[i], 0, S)
             if i == last:
                 break
             theirs = values[i][:].bitcast(BF16)[:, 0:M]

@@ -179,10 +179,11 @@ def tile_list_merge_conflict_scores_kernel(
             )
             wv_codes[i], wv_plane[i] = codes, plane
 
-        gates, values = {}, {}
+        sigs, gates, values = {}, {}, {}
 
         def products(i):
-            sig = ring.tile([P, S], F32, name="sig")
+            sig = ring.tile([P, S], F32, name="sig", bufs=3, align_bytes=64)
+            sigs[i] = sig
             value = ring.tile([P, S], F32, name="value", align_bytes=64)
             halves = [slice(h * BANK, (h + 1) * BANK) for h in range(S // BANK)]
             pre = [psum.tile([P, BANK], F32, name="pre", tag="acc", bufs=4) for h in halves]
@@ -326,7 +327,7 @@ def tile_list_merge_conflict_scores_kernel(
                 scatter(i, gates[i], 0, S)
             if i == last:
                 break
-            theirs = values[i][:].bitcast(BF16)[:, 0:M]
+            theirs = sigs[i][:, BANK:].bitcast(BF16)
             if i > 0:
                 fetch(theirs, i - 1, idx4, 0, M)
             ours[i] = ring.tile([P, M], BF16, name="ours")
@@ -346,8 +347,8 @@ def tile_list_merge_conflict_scores_kernel(
                     turn_second(0, c, first_pass[:, PACK * STARTS[c] : PACK * (STARTS[c] + WIDTHS[c])], "scalar")
 
         slot_cols = PACK * max(WIDTHS)
-        spent = [values[last][:].bitcast(BF16), gates[last][:].bitcast(BF16)]
-        stage = [spent[s // 2][:, (s % 2) * slot_cols : (s % 2 + 1) * slot_cols] for s in range(SLOTS)]
+        spent = values[last][:].bitcast(BF16)
+        stage = [sigs[last][:, BANK:].bitcast(BF16), spent[:, :slot_cols], spent[:, slot_cols:]]
 
         def finish(c):
             if c >= EARLY:

@@ -68,8 +68,6 @@ def tile_list_merge_conflict_scores_kernel(
         nc.vector.memset(tab_plane[:].bitcast(I32), 0)
         bg_rows = keep.tile([P, P], F32)
         nc.vector.memset(bg_rows[:], 0.0)
-        warm = keep.tile([P, 1], F32)
-        nc.scalar.activation(warm[:], bg_rows[:, P - 1 : P], SIGMOID)
         v_plane = [keep.tile([P, S], U8, name="v_plane%d" % a, align_bytes=64) for a in range(PASSES)]
         nc.vector.memset(v_plane[1][:].bitcast(I32), 0)
         w4_plane = keep.tile([P, PASSES, H], U8, align_bytes=64)

@@ -16,7 +16,9 @@ FP8X4 = mybir.dt.float8_e4m3fn_x4
 FP4X4 = mybir.dt.float4_e2m1fn_x4
 MULT = mybir.AluOpType.mult
 MAX = mybir.AluOpType.max
+SUBTRACT = mybir.AluOpType.subtract
 SIGMOID = mybir.ActivationFunctionType.Sigmoid
+RELU = mybir.ActivationFunctionType.Relu
 
 P = 128
 PACK = 4
@@ -31,8 +33,10 @@ N_TILES = N // P
 LIST = 16
 W4_HEAD = 2
 AHEAD = 3
+LAG = 2
 EARLY = 2
 SLOTS = 3
+PIECE = 256
 
 
 def tile_list_merge_conflict_scores_kernel(
@@ -44,6 +48,7 @@ def tile_list_merge_conflict_scores_kernel(
         lists = ctx.enter_context(tc.tile_pool(name="lists", bufs=1))
         keep = ctx.enter_context(tc.tile_pool(name="keep", bufs=1))
         ring = ctx.enter_context(tc.tile_pool(name="ring", bufs=2))
+        shared = ctx.enter_context(tc.tile_pool(name="shared", bufs=1))
         psum = ctx.enter_context(tc.psum_pool(name="psum", bufs=2))
 
         def load_list(src, name):
@@ -54,8 +59,8 @@ def tile_list_merge_conflict_scores_kernel(
         def entries(tile, first, count):
             return tile[:, first // LIST : (first + count) // LIST]
 
-        def zero_plane(engine, plane):
-            engine.memset(plane[:].rearrange("p a c -> p (a c)").bitcast(I32), 0)
+        def zero_plane(plane):
+            nc.vector.memset(plane[:].rearrange("p a c -> p (a c)").bitcast(I32), 0)
 
         def load_plane(queue, plane, scales):
             for q in range(4):
@@ -64,39 +69,36 @@ def tile_list_merge_conflict_scores_kernel(
                     scales.bitcast(I32)[:, 4 * q : 4 * q + 4, :].rearrange("a r c -> r a c"),
                 )
 
-        tab_plane = keep.tile([P, T], U8, align_bytes=64)
+        def move(engine, dst, src):
+            if engine == "vector":
+                nc.vector.tensor_copy(dst, src)
+            else:
+                nc.scalar.copy(dst, src)
+
+        tab_plane = shared.tile([P, T], U8, offset=2048, align_bytes=64)
         nc.vector.memset(tab_plane[:].bitcast(I32), 0)
+        for q in range(4):
+            nc.gpsimd.dma_start(
+                tab_plane[:].bitcast(I32)[32 * q : 32 * q + 4 * PASSES, :],
+                tab_scales.bitcast(I32)[:, 4 * q : 4 * q + 4, :],
+            )
+        w4_plane = keep.tile([P, PASSES, H], U8, align_bytes=64)
+        zero_plane(w4_plane)
+        load_plane(nc.gpsimd, w4_plane, w4_scales)
         bg_rows = keep.tile([P, P], F32)
         nc.vector.memset(bg_rows[:], 0.0)
         v_plane = [keep.tile([P, S], U8, name="v_plane%d" % a, align_bytes=64) for a in range(PASSES)]
         nc.vector.memset(v_plane[1][:].bitcast(I32), 0)
-        w4_plane = keep.tile([P, PASSES, H], U8, align_bytes=64)
-        zero_plane(nc.gpsimd, w4_plane)
-        load_plane(nc.gpsimd, w4_plane, w4_scales)
+        w8_plane = keep.tile([P, PASSES, N], U8, align_bytes=64)
+        zero_plane(w8_plane)
         ident_f32 = keep.tile([P, P], F32)
         make_identity(nc, ident_f32[:])
         ident_bf16 = keep.tile([P, P], BF16)
-        make_identity(nc, ident_bf16[:])
-        w8_plane = keep.tile([P, PASSES, N], U8, align_bytes=64)
-        zero_plane(nc.gpsimd, w8_plane)
-
-        tab = [keep.tile([P, T], I32, name="tab%d" % a) for a in range(PASSES)]
-        tab_src = [tab_words[a].rearrange("p t i -> p (t i)").bitcast(I32) for a in range(PASSES)]
-        nc.sync.dma_start(tab[0][:, : T // 4], tab_src[0][:, : T // 4])
-        for q in range(4):
-            nc.sync.dma_start(
-                tab_plane[:].bitcast(I32)[32 * q : 32 * q + 4 * PASSES, :],
-                tab_scales.bitcast(I32)[:, 4 * q : 4 * q + 4, :],
-            )
-        idx = load_list(offs, "idx")
-        nc.sync.dma_start(tab[0][:, T // 4 :], tab_src[0][:, T // 4 :])
-        nc.sync.dma_start(tab[1][:, : T // 2], tab_src[1][:, : T // 2])
-        nc.sync.dma_start(bg_rows[0:ROW_TILES, :], bg.rearrange("(i p) -> i p", p=P))
+        nc.scalar.copy(ident_bf16[:], ident_f32[:])
 
         w4_src = w4_words.bitcast(I32).rearrange("a p c -> p a c")
         head_words = W4_HEAD * P // 2
         w4_head = keep.tile([P, PASSES, 4 * head_words], U8, align_bytes=64)
-        nc.sync.dma_start(w4_head[:].bitcast(I32), w4_src[:, :, 0:head_words])
         w4_rest = keep.tile([P, PASSES, 2 * H - 4 * head_words], U8, align_bytes=64)
 
         def w4_codes(a, i):
@@ -104,85 +106,104 @@ def tile_list_merge_conflict_scores_kernel(
                 return w4_head[:, a, 2 * P * i : 2 * P * (i + 1)]
             return w4_rest[:, a, 2 * P * (i - W4_HEAD) : 2 * P * (i - W4_HEAD + 1)]
 
-        def move(engine, dst, src):
-            if engine == "vector":
-                nc.vector.tensor_copy(dst, src)
-            else:
-                nc.scalar.copy(dst, src)
+        wv_raw = [keep.tile([P, PASSES * PACK * P], F32, name="wv_raw%d" % i, align_bytes=64) for i in range(ROW_TILES)]
+        pages = {}
 
-        wv_raw, pages = {}, {}
+        def raw_pass(i, a):
+            return wv_raw[i][:, a * PACK * P : (a + 1) * PACK * P].rearrange("p (j c) -> p j c", j=PACK)
 
         def load_wv_pass(i, a):
-            if a == 0:
-                wv_raw[i] = ring.tile([P, PASSES, PACK, P], F32, name="wv_raw", bufs=3)
             rows = wv[a * P * PACK : (a + 1) * P * PACK, i * P : (i + 1) * P]
-            nc.sync.dma_start(wv_raw[i][:, a, :, :], rows.rearrange("(p j) c -> p j c", j=PACK))
+            nc.sync.dma_start(raw_pass(i, a), rows.rearrange("(p j) c -> p j c", j=PACK))
 
         def load_wv(i):
             for a in range(PASSES):
                 load_wv_pass(i, a)
 
         def load_page(i):
-            page = ring.tile([P, T2], F32, name="page", bufs=4)
+            page = ring.tile([P, T2], F32, name="page", bufs=5)
             nc.sync.dma_start(page[:], page0[i * P : (i + 1) * P, :])
             pages[i] = page
 
+        tab = [shared.tile([P, T], I32, name="tab%d" % a, offset=(6144, 24576)[a], align_bytes=64) for a in range(PASSES)]
+        tab_src = [tab_words[a].rearrange("p t i -> p (t i)").bitcast(I32) for a in range(PASSES)]
+        idx = load_list(offs, "idx")
+        nc.sync.dma_start(tab[0][:], tab_src[0])
+        nc.sync.dma_start(w4_head[:].bitcast(I32), w4_src[:, :, 0:head_words])
+        idx2 = load_list(offs2, "idx2")
         load_wv(0)
-        nc.sync.dma_start(tab[1][:, T // 2 :], tab_src[1][:, T // 2 :])
+        nc.sync.dma_start(tab[1][:], tab_src[1])
+        nc.scalar.dma_start(bg_rows[0:ROW_TILES, :], bg.rearrange("(i p) -> i p", p=P))
         gains = keep.tile([P, S], F32)
         nc.sync.dma_start(gains[:, :BANK], wgs[:, :BANK])
+        load_wv_pass(1, 0)
         load_page(0)
-        idx2 = load_list(offs2, "idx2")
-        load_wv(1)
-        load_wv_pass(2, 0)
+        load_wv_pass(1, 1)
         nc.sync.dma_start(gains[:, BANK:], wgs[:, BANK:])
-        load_wv_pass(2, 1)
+        load_wv(2)
+        load_page(1)
+        nc.sync.dma_start(w4_rest[:].bitcast(I32), w4_src[:, :, head_words:])
         idx3 = load_list(offs3, "idx3")
         idx4 = load_list(offs4, "idx4")
-        nc.sync.dma_start(w4_rest[:].bitcast(I32), w4_src[:, :, head_words:])
+        load_wv(3)
+        load_wv(4)
+        load_page(2)
+        load_wv(5)
+        load_page(3)
+        load_wv(6)
+        load_wv(7)
+        load_page(4)
+        w8_codes = keep.tile([P, PASSES, N], I32, align_bytes=64)
+        nc.sync.dma_start(w8_codes[:], w8_words.rearrange("a p c i -> p a (c i)").bitcast(I32))
+        load_plane(nc.sync, w8_plane, w8_scales)
 
         bg_turned = psum.tile([P, P], F32, name="turn2")
         nc.tensor.transpose(bg_turned[:], bg_rows[:], ident_f32[:])
         bias = keep.tile([P, ROW_TILES], F32)
         nc.scalar.copy(bias[:], bg_turned[:, 0:ROW_TILES])
 
-        v_codes = [keep.tile([P, S], U32, name="v_codes%d" % a, align_bytes=64) for a in range(PASSES)]
+        v_codes = [shared.tile([P, S], U32, name="v_codes%d" % a, offset=4096 * a, align_bytes=64) for a in range(PASSES)]
         nc.vector.tensor_copy(v_plane[0][:], tab_plane[:].indirect(idx[:]))
-        nc.scalar.dma_start(v_plane[1][:].bitcast(I32)[0:100, :], v_plane[0][:].bitcast(I32)[4:104, :])
+        nc.gpsimd.dma_start(v_plane[1][:].bitcast(I32)[0:100, :], v_plane[0][:].bitcast(I32)[4:104, :])
         nc.vector.tensor_copy(v_codes[0][:], tab[0][:].bitcast(U32).indirect(idx[:]))
-        for h in range(S // BANK):
-            nc.vector.tensor_copy(
-                v_codes[1][:, h * BANK : (h + 1) * BANK],
-                tab[1][:].bitcast(U32).indirect(entries(idx, h * BANK, BANK)),
-            )
 
-        wv_grouped, wv_codes, wv_plane = {}, {}, {}
-
-        def group_wv(i):
-            grouped = ring.tile([P, PASSES, P, PACK], BF16, name="wv_grouped", align_bytes=64)
-            for a in range(PASSES):
-                nc.scalar.copy(
-                    grouped[:, a, :, :].rearrange("p (c e) j -> p c j e", e=4),
-                    wv_raw[i][:, a, :, :].rearrange("p j (c e) -> p c j e", e=4),
+        def gather_second_pass():
+            for h in range(S // BANK):
+                nc.vector.tensor_copy(
+                    v_codes[1][:, h * BANK : (h + 1) * BANK],
+                    tab[1][:].bitcast(U32).indirect(entries(idx, h * BANK, BANK)),
                 )
-            wv_grouped[i] = grouped
 
-        def quantize_wv(i):
-            codes = ring.tile([P, PASSES * P], U32, name="wv_codes", bufs=4, align_bytes=64)
-            plane = ring.tile([P, PASSES * P], U8, name="wv_plane", bufs=4, align_bytes=64)
+        width = PASSES * P
+        wv_codes = keep.tile([P, ROW_TILES * width], U32, align_bytes=64)
+        wv_plane = keep.tile([P, ROW_TILES * width], U8, align_bytes=64)
+
+        def quantize_wv(first, count, grouped):
+            for e in range(count):
+                for a in range(PASSES):
+                    start = (e * PASSES + a) * P * PACK
+                    nc.scalar.copy(
+                        grouped[:, start : start + P * PACK].rearrange("p (c e j) -> p c j e", e=4, j=PACK),
+                        raw_pass(first + e, a).rearrange("p j (c e) -> p c j e", e=4),
+                    )
+            cols = slice(first * width, (first + count) * width)
             nc.vector.quantize_mx(
-                out=codes[:].bitcast(FP8X4),
-                scales=plane[:],
-                in_=wv_grouped[i][:].rearrange("p a c j -> p (a c j)"),
+                out=wv_codes[:, cols].bitcast(FP8X4), scales=wv_plane[:, cols], in_=grouped[:, 0 : count * width * PACK]
             )
-            wv_codes[i], wv_plane[i] = codes, plane
 
-        sigs, gates, values = {}, {}, {}
+        sigs, gates, values, placed = {}, {}, {}, {}
 
-        def products(i):
-            sig = ring.tile([P, S], F32, name="sig", bufs=3, align_bytes=64)
-            sigs[i] = sig
-            value = ring.tile([P, S], F32, name="value", align_bytes=64)
+        def make_gate(i, cols):
+            nc.gpsimd.tensor_tensor(gates[i][:, cols], sigs[i][:, cols], gains[:, cols], MULT)
+
+        def make_placed(i, cols, dst):
+            nc.gpsimd.tensor_tensor(dst, gates[i][:, cols], values[i][:, cols], MULT)
+
+        def products(i, piece):
+            sig = ring.tile([P, S], F32, name="sig", align_bytes=64)
+            gate = ring.tile([P, S], F32, name="gate", align_bytes=64)
+            value = ring.tile([P, S], F32, name="value", bufs=3, align_bytes=64)
+            done = ring.tile([P, S], F32, name="placed", align_bytes=64)
             halves = [slice(h * BANK, (h + 1) * BANK) for h in range(S // BANK)]
             pre = [psum.tile([P, BANK], F32, name="pre", tag="acc", bufs=4) for h in halves]
             lin = [psum.tile([P, BANK], F32, name="lin", tag="acc", bufs=4) for h in halves]
@@ -198,62 +219,75 @@ def tile_list_merge_conflict_scores_kernel(
                     stop=(a == PASSES - 1),
                 )
 
-            def pre_pass(a, h):
+            def both(a, h):
                 one_pass(pre[h], w4_codes(a, i).bitcast(FP4X4), w4_plane[:, a, i * P : (i + 1) * P], a, halves[h])
+                cols = slice(i * width + a * P, i * width + (a + 1) * P)
+                one_pass(lin[h], wv_codes[:, cols].bitcast(FP8X4), wv_plane[:, cols], a, halves[h])
 
-            def lin_pass(a, h):
-                cols = slice(a * P, (a + 1) * P)
-                one_pass(lin[h], wv_codes[i][:, cols].bitcast(FP8X4), wv_plane[i][:, cols], a, halves[h])
-
-            for h in range(len(halves)):
-                pre_pass(0, h)
-            for h in range(len(halves)):
-                lin_pass(0, h)
-            for h in range(len(halves)):
-                pre_pass(1, h)
-                lin_pass(1, h)
+            order = [(a, h) for h in range(len(halves)) for a in range(PASSES)]
             if i == 0:
-                for h, cols in enumerate(halves):
-                    nc.scalar.activation(sig[:, cols], pre[h][:], SIGMOID, bias=bias[:, i : i + 1])
-                    first, second = (sig, gains) if h == 0 else (gains, sig)
-                    nc.vector.tensor_tensor(value[:, cols], lin[h][:], first[:, cols], MULT)
-                    gates[i, h] = second
-                values[i] = value
-                return
-            gate = ring.tile([P, S], F32, name="gate", align_bytes=64)
-            for h, cols in enumerate(halves):
-                nc.scalar.activation(sig[:, cols], pre[h][:], SIGMOID, bias=bias[:, i : i + 1])
-                nc.gpsimd.tensor_tensor(gate[:, cols], sig[:, cols], gains[:, cols], MULT)
-            for h, cols in enumerate(halves):
-                nc.scalar.copy(value[:, cols], lin[h][:])
-            gates[i], values[i] = gate, value
+                order = [(a, h) for a in range(PASSES) for h in range(len(halves))]
+            for a, h in order:
+                both(a, h)
+            sigs[i], gates[i], values[i], placed[i] = sig, gate, value, done
+            for first in range(0, S, piece):
+                h, local = divmod(first, BANK)
+                cols, bank_cols = slice(first, first + piece), slice(local, local + piece)
+                nc.scalar.activation(sig[:, cols], pre[h][:, bank_cols], SIGMOID, bias=bias[:, i : i + 1])
+                nc.scalar.copy(value[:, cols], lin[h][:, bank_cols])
+                make_gate(i, cols)
+                if i > 0 or h == 0:
+                    make_placed(i, cols, done[:, cols])
 
-        def scatter(i, gate, first, count):
-            cols = slice(first, first + count)
-            nc.vector.tensor_tensor(
-                pages[i][:].indirect(entries(idx2, first, count)), values[i][:, cols], gate[:, cols], MULT
-            )
+        def scatter_from(i, first, count, src):
+            nc.vector.tensor_copy(pages[i][:].indirect(entries(idx2, first, count)), src)
+
+        def scatter(i, first, count):
+            scatter_from(i, first, count, placed[i][:, first : first + count])
 
         def fetch(dst, i, lst, first, count):
             nc.vector.tensor_copy(dst, pages[i][:].indirect(entries(lst, first, count)))
 
-        z_rows = [
-            [keep.tile([P, w // P, P * PACK], BF16, name="z_rows%d_%d" % (a, c)) for c, w in enumerate(WIDTHS)]
-            for a in range(PASSES)
-        ]
+        rows0_tile = shared.tile([P, M * PACK], BF16, offset=8192, align_bytes=64)
+        rows0 = rows0_tile[:].rearrange("p (b r) -> p b r", r=P * PACK)
+        first_pass_tile = shared.tile([P, M * PACK], BF16, offset=16384, align_bytes=64)
+        first_pass = first_pass_tile[:]
+        rows1 = [keep.tile([P, w // P, P * PACK], BF16, name="rows1_%d" % c) for c, w in enumerate(WIDTHS)]
 
-        def turn_first(i, c, tiles, engine):
+        theirs = {}
+
+        def difference(i, dst):
+            nc.vector.tensor_tensor(dst[:], pages[i][:].indirect(idx3[:]), theirs[i][:], SUBTRACT)
+            excess = ring.tile([P, M], F32, name="excess", align_bytes=64)
             a, slot = divmod(i, TILES_PER_PASS)
+            r_cols = slice(slot * P, (slot + 1) * P)
+            for h in range(M // BANK):
+                cols = slice(h * BANK, (h + 1) * BANK)
+                nc.scalar.activation(excess[:, cols], dst[:, cols], RELU)
+            for h in range(M // BANK):
+                turned = psum.tile([P, BANK // P, P], F32, name="turn1")
+                for b in range(BANK // P):
+                    cols = slice(h * BANK + b * P, h * BANK + (b + 1) * P)
+                    nc.tensor.matmul(turned[:, b, :], theirs[i][:, cols], ident_f32[:], start=True, stop=False, is_transpose=True)
+                    nc.tensor.matmul(turned[:, b, :], excess[:, cols], ident_f32[:], start=False, stop=True, is_transpose=True)
+                if a == 0:
+                    nc.scalar.copy(rows0[:, h * BANK // P : (h + 1) * BANK // P, r_cols], turned[:])
+                else:
+                    for c in range(CHUNKS):
+                        if STARTS[c] // BANK == h:
+                            b0 = (STARTS[c] - h * BANK) // P
+                            nc.scalar.copy(rows1[c][:, :, r_cols], turned[:, b0 : b0 + WIDTHS[c] // P, :])
+
+        def turn_first(c, tiles, engine):
+            slot = TILES_PER_PASS - len(tiles)
             blocks = WIDTHS[c] // P
             turned = psum.tile([P, blocks, len(tiles), P], BF16, name="turn1")
             for e, z in enumerate(tiles):
                 for b in range(blocks):
                     nc.tensor.transpose(turned[:, b, e, :], z[:, b * P : (b + 1) * P], ident_bf16[:])
-            move(engine, z_rows[a][c][:, :, slot * P : (slot + len(tiles)) * P], turned[:].rearrange("p b e r -> p b (e r)"))
+            move(engine, rows1[c][:, :, slot * P :], turned[:].rearrange("p b e r -> p b (e r)"))
 
-        def turn_second(a, c, grouped, engine):
-            blocks = WIDTHS[c] // P
-            words = z_rows[a][c][:].bitcast(F32)
+        def turn_second(words, blocks, grouped, engine):
             turned = psum.tile([P, blocks, 2, P], F32, name="turn2")
             for b in range(blocks):
                 for u in range(2):
@@ -273,7 +307,6 @@ def tile_list_merge_conflict_scores_kernel(
         def quantize_z(a, cols, grouped):
             nc.vector.quantize_mx(out=z_codes[a][:, cols].bitcast(FP8X4), scales=z_plane[a][:, cols], in_=grouped)
 
-        w8_codes = keep.tile([P, PASSES, N], I32, align_bytes=64)
         sums = {}
 
         def score_pass(a, c):
@@ -293,60 +326,66 @@ def tile_list_merge_conflict_scores_kernel(
                     )
 
         out_tiles = out.rearrange("(t p) m -> p t m", p=P)
+        staged = shared.tile([P, N_TILES * M], F32, offset=24576, align_bytes=64)
 
         def store_scores(c):
             for pair in range(N_TILES // 2):
-                staged = ring.tile([P, 2, WIDTHS[c]], F32, name="staged", bufs=2 * CHUNKS)
-                move("vector" if c >= EARLY and pair == 1 else "scalar", staged[:], sums[c, pair][:])
-                nc.sync.dma_start(out_tiles[:, 2 * pair : 2 * pair + 2, chunk(c)], staged[:])
+                first = N_TILES * STARTS[c] + pair * 2 * WIDTHS[c]
+                piece = staged[:, first : first + 2 * WIDTHS[c]].rearrange("p (e m) -> p e m", e=2)
+                move("vector" if c >= EARLY and pair == 1 else "scalar", piece, sums[c, pair][:])
+                nc.sync.dma_start(out_tiles[:, 2 * pair : 2 * pair + 2, chunk(c)], piece)
 
-        group_wv(0)
-        quantize_wv(0)
-        products(0)
-        scatter(0, gates[0, 0], 0, BANK)
-        for i in range(1, AHEAD):
-            group_wv(i)
-            quantize_wv(i)
+        grouped0 = shared.tile([P, width * PACK], BF16, offset=4096, align_bytes=64)
+        quantize_wv(0, 1, grouped0[:])
+        gather_second_pass()
+        products(0, PIECE)
+        scatter(0, 0, PIECE)
+        scatter(0, PIECE, PIECE)
+        quantize_wv(1, 1, values[0][:, :BANK].bitcast(BF16))
+        make_placed(0, slice(2 * PIECE, 3 * PIECE), wv_raw[1][:, :PIECE])
+        scatter_from(0, 2 * PIECE, PIECE, wv_raw[1][:, :PIECE])
+        quantize_wv(2, 1, sigs[0][:, BANK:].bitcast(BF16))
+        make_placed(0, slice(3 * PIECE, 4 * PIECE), wv_raw[2][:, :PIECE])
+        scatter_from(0, 3 * PIECE, PIECE, wv_raw[2][:, :PIECE])
+        products(1, BANK)
+        theirs[0] = wv_raw[0]
+        fetch(theirs[0][:], 0, idx4, 0, M)
+        products(2, BANK)
+
         last = ROW_TILES - 1
-        ours = {}
-        first_pass = keep.tile([P, M * PACK], BF16, align_bytes=64)
-        for i in range(ROW_TILES):
-            if i + AHEAD < ROW_TILES:
-                load_wv(i + AHEAD)
-            if i < last:
-                load_page(i + 1)
-                products(i + 1)
+        for i in range(1, last):
             if i == 1:
-                nc.sync.dma_start(w8_codes[:], w8_words.rearrange("a p c i -> p a (c i)").bitcast(I32))
-                load_plane(nc.sync, w8_plane, w8_scales)
-            if i == 0:
-                scatter(i, gates[0, 1], BANK, BANK)
+                for first in range(0, S, BANK):
+                    scatter(i, first, BANK)
             else:
-                scatter(i, gates[i], 0, S)
-            if i == last:
-                break
-            theirs = sigs[i][:, BANK:].bitcast(BF16)
-            if i > 0:
-                fetch(theirs, i - 1, idx4, 0, M)
-            ours[i] = ring.tile([P, M], BF16, name="ours")
-            fetch(ours[i][:], i, idx3, 0, M)
-            if i + AHEAD < ROW_TILES:
-                group_wv(i + AHEAD)
-                quantize_wv(i + AHEAD)
-            if i == TILES_PER_PASS + 1:
-                quantize_z(0, slice(0, M), first_pass[:])
-            if i > 0:
-                best = ring.tile([P, M], BF16, name="best")
-                nc.vector.tensor_tensor(best[:], ours[i - 1][:], theirs, MAX)
-                for c in range(CHUNKS):
-                    turn_first(i - 1, c, [best[:, chunk(c)]], "scalar")
-            if i == TILES_PER_PASS:
-                for c in range(CHUNKS):
-                    turn_second(0, c, first_pass[:, PACK * STARTS[c] : PACK * (STARTS[c] + WIDTHS[c])], "scalar")
+                scatter(i, 0, S)
+            if i >= LAG:
+                difference(i - LAG, gates[i])
+                if i + AHEAD < ROW_TILES:
+                    load_page(i + AHEAD)
+            if i == 1:
+                quantize_wv(AHEAD, 2, values[i][:].bitcast(BF16))
+            elif i + AHEAD < ROW_TILES:
+                quantize_wv(i + AHEAD, 1, values[i][:].bitcast(BF16))
+            if i == last - 1:
+                ours = keep.tile([P, M], BF16, align_bytes=64)
+                fetch(ours[:], i, idx3, 0, M)
+            else:
+                theirs[i] = wv_raw[i + AHEAD] if i + AHEAD < ROW_TILES else wv_raw[1]
+                fetch(theirs[i][:], i, idx4, 0, M)
+            if i + LAG < ROW_TILES:
+                products(i + LAG, BANK)
+            if i == TILES_PER_PASS - 1 + LAG:
+                words = rows0.bitcast(F32)
+                for b in range(0, M // P, 2):
+                    turn_second(words[:, b : b + 2, :], 2, first_pass[:, PACK * P * b : PACK * P * (b + 2)], "scalar")
+        quantize_z(0, slice(0, M), first_pass)
+        difference(last - LAG, gates[last])
+        scatter(last, 0, S)
 
         slot_cols = PACK * max(WIDTHS)
-        spent = values[last][:].bitcast(BF16)
-        stage = [sigs[last][:, BANK:].bitcast(BF16), spent[:, :slot_cols], spent[:, slot_cols:]]
+        spent = placed[last][:].bitcast(BF16)
+        stage = [values[last][:, BANK:].bitcast(BF16), spent[:, :slot_cols], spent[:, slot_cols:]]
 
         def finish(c):
             if c >= EARLY:
@@ -366,10 +405,10 @@ def tile_list_merge_conflict_scores_kernel(
             fetch(slots[1], last, idx3, STARTS[c], w)
             fetch(slots[2], last, idx4, STARTS[c], w)
             best = ring.tile([P, 2, w], BF16, name="best")
-            nc.vector.tensor_tensor(best[:, 0, :], ours[last - 1][:, chunk(c)], slots[0], MAX)
+            nc.vector.tensor_tensor(best[:, 0, :], ours[:, chunk(c)], slots[0], MAX)
             nc.vector.tensor_tensor(best[:, 1, :], slots[1], slots[2], MAX)
             engine = "vector" if c == CHUNKS - 1 else "scalar"
-            turn_first(last - 1, c, [best[:, 0, :], best[:, 1, :]], engine)
-            turn_second(1, c, stage[c % SLOTS][:, 0 : PACK * w], engine)
+            turn_first(c, [best[:, 0, :], best[:, 1, :]], engine)
+            turn_second(rows1[c][:].bitcast(F32), w // P, stage[c % SLOTS][:, 0 : PACK * w], engine)
         for c in range(CHUNKS - SLOTS, CHUNKS):
             finish(c)

@@ -26,7 +26,7 @@ PASSES = 2
 BANK = 512
 ROW_TILES = H // P
 TILES_PER_PASS = ROW_TILES // PASSES
-WIDTHS = [256, 256, 256, 128, 128]
+WIDTHS = [128, 256, 256, 256, 128]
 STARTS = [sum(WIDTHS[:c]) for c in range(len(WIDTHS))]
 CHUNKS = len(WIDTHS)
 N_TILES = N // P
@@ -34,8 +34,11 @@ LIST = 16
 W4_HEAD = 2
 AHEAD = 3
 LAG = 2
-EARLY = 2
-SLOTS = 3
+EARLY = 3
+SCORE_BANKS = 5
+SLOTS = 2
+PINNED = 0
+ON_VECTOR = [(2, 1), (3, 1), (4, 0)]
 PIECE = 256
 
 
@@ -49,7 +52,11 @@ def tile_list_merge_conflict_scores_kernel(
         keep = ctx.enter_context(tc.tile_pool(name="keep", bufs=1))
         ring = ctx.enter_context(tc.tile_pool(name="ring", bufs=2))
         shared = ctx.enter_context(tc.tile_pool(name="shared", bufs=1))
-        psum = ctx.enter_context(tc.psum_pool(name="psum", bufs=2))
+        psum = ctx.enter_context(tc.psum_pool(name="psum", bufs=1))
+
+        def bank(number, shape, dtype, name):
+            return psum.tile(shape, dtype, name="%s_bank%d" % (name, number), offset=2048 * number)
+
 
         def load_list(src, name):
             tile = lists.tile([P, S // LIST], U16, name=name)
@@ -75,26 +82,28 @@ def tile_list_merge_conflict_scores_kernel(
             else:
                 nc.scalar.copy(dst, src)
 
-        tab_plane = shared.tile([P, T], U8, offset=2048, align_bytes=64)
-        nc.vector.memset(tab_plane[:].bitcast(I32), 0)
-        for q in range(4):
-            nc.gpsimd.dma_start(
-                tab_plane[:].bitcast(I32)[32 * q : 32 * q + 4 * PASSES, :],
-                tab_scales.bitcast(I32)[:, 4 * q : 4 * q + 4, :],
-            )
+        tab_plane = [keep.tile([P, T], U8, name="tab_plane%d" % a, align_bytes=64) for a in range(PASSES)]
+        for a in range(PASSES):
+            nc.vector.memset(tab_plane[a][:].bitcast(I32), 0)
+
+        def load_tab_plane(a):
+            for q in range(4):
+                nc.sync.dma_start(
+                    tab_plane[a][:].bitcast(I32)[32 * q : 32 * q + 4, :], tab_scales.bitcast(I32)[a, 4 * q : 4 * q + 4, :]
+                )
+
         w4_plane = keep.tile([P, PASSES, H], U8, align_bytes=64)
-        zero_plane(w4_plane)
+        nc.gpsimd.memset(w4_plane[:].rearrange("p a c -> p (a c)").bitcast(I32), 0)
         load_plane(nc.gpsimd, w4_plane, w4_scales)
         bg_rows = keep.tile([P, P], F32)
         nc.vector.memset(bg_rows[:], 0.0)
         v_plane = [keep.tile([P, S], U8, name="v_plane%d" % a, align_bytes=64) for a in range(PASSES)]
-        nc.vector.memset(v_plane[1][:].bitcast(I32), 0)
         w8_plane = keep.tile([P, PASSES, N], U8, align_bytes=64)
         zero_plane(w8_plane)
         ident_f32 = keep.tile([P, P], F32)
         make_identity(nc, ident_f32[:])
         ident_bf16 = keep.tile([P, P], BF16)
-        nc.scalar.copy(ident_bf16[:], ident_f32[:])
+        nc.scalar.activation(ident_bf16[:], ident_f32[:], SIGMOID, scale=2000.0, bias=-1000.0)
 
         w4_src = w4_words.bitcast(I32).rearrange("a p c -> p a c")
         head_words = W4_HEAD * P // 2
@@ -125,15 +134,19 @@ def tile_list_merge_conflict_scores_kernel(
             nc.sync.dma_start(page[:], page0[i * P : (i + 1) * P, :])
             pages[i] = page
 
-        tab = [shared.tile([P, T], I32, name="tab%d" % a, offset=(6144, 24576)[a], align_bytes=64) for a in range(PASSES)]
+        tab = [shared.tile([P, T], I32, name="tab%d" % a, offset=16384 * a, align_bytes=64) for a in range(PASSES)]
         tab_src = [tab_words[a].rearrange("p t i -> p (t i)").bitcast(I32) for a in range(PASSES)]
+        nc.sync.dma_start(tab[0][:, : T // 4], tab_src[0][:, : T // 4])
+        load_tab_plane(0)
         idx = load_list(offs, "idx")
-        nc.sync.dma_start(tab[0][:], tab_src[0])
+        nc.sync.dma_start(tab[0][:, T // 4 :], tab_src[0][:, T // 4 :])
         nc.sync.dma_start(w4_head[:].bitcast(I32), w4_src[:, :, 0:head_words])
-        idx2 = load_list(offs2, "idx2")
         load_wv(0)
-        nc.sync.dma_start(tab[1][:], tab_src[1])
-        nc.scalar.dma_start(bg_rows[0:ROW_TILES, :], bg.rearrange("(i p) -> i p", p=P))
+        load_tab_plane(1)
+        nc.sync.dma_start(bg_rows[0:ROW_TILES, :], bg.rearrange("(i p) -> i p", p=P))
+        for h in range(2):
+            nc.sync.dma_start(tab[1][:, h * T // 2 : (h + 1) * T // 2], tab_src[1][:, h * T // 2 : (h + 1) * T // 2])
+        idx2 = load_list(offs2, "idx2")
         gains = keep.tile([P, S], F32)
         nc.sync.dma_start(gains[:, :BANK], wgs[:, :BANK])
         load_wv_pass(1, 0)
@@ -157,15 +170,15 @@ def tile_list_merge_conflict_scores_kernel(
         nc.sync.dma_start(w8_codes[:], w8_words.rearrange("a p c i -> p a (c i)").bitcast(I32))
         load_plane(nc.sync, w8_plane, w8_scales)
 
-        bg_turned = psum.tile([P, P], F32, name="turn2")
+        bg_turned = bank(7, [P, P], F32, "bias")
         nc.tensor.transpose(bg_turned[:], bg_rows[:], ident_f32[:])
         bias = keep.tile([P, ROW_TILES], F32)
         nc.scalar.copy(bias[:], bg_turned[:, 0:ROW_TILES])
 
-        v_codes = [shared.tile([P, S], U32, name="v_codes%d" % a, offset=4096 * a, align_bytes=64) for a in range(PASSES)]
-        nc.vector.tensor_copy(v_plane[0][:], tab_plane[:].indirect(idx[:]))
-        nc.gpsimd.dma_start(v_plane[1][:].bitcast(I32)[0:100, :], v_plane[0][:].bitcast(I32)[4:104, :])
+        v_codes = [keep.tile([P, S], U32, name="v_codes%d" % a, align_bytes=64) for a in range(PASSES)]
+        nc.vector.tensor_copy(v_plane[0][:], tab_plane[0][:].indirect(idx[:]))
         nc.vector.tensor_copy(v_codes[0][:], tab[0][:].bitcast(U32).indirect(idx[:]))
+        nc.vector.tensor_copy(v_plane[1][:], tab_plane[1][:].indirect(idx[:]))
 
         def gather_second_pass():
             for h in range(S // BANK):
@@ -205,8 +218,8 @@ def tile_list_merge_conflict_scores_kernel(
             value = ring.tile([P, S], F32, name="value", bufs=3, align_bytes=64)
             done = ring.tile([P, S], F32, name="placed", align_bytes=64)
             halves = [slice(h * BANK, (h + 1) * BANK) for h in range(S // BANK)]
-            pre = [psum.tile([P, BANK], F32, name="pre", tag="acc", bufs=4) for h in halves]
-            lin = [psum.tile([P, BANK], F32, name="lin", tag="acc", bufs=4) for h in halves]
+            pre = [bank(2 * h, [P, BANK], F32, "pre") for h in range(len(halves))]
+            lin = [bank(2 * h + 1, [P, BANK], F32, "lin") for h in range(len(halves))]
 
             def one_pass(acc, codes, plane, a, cols):
                 nc.tensor.matmul_mx(
@@ -234,6 +247,10 @@ def tile_list_merge_conflict_scores_kernel(
                 h, local = divmod(first, BANK)
                 cols, bank_cols = slice(first, first + piece), slice(local, local + piece)
                 nc.scalar.activation(sig[:, cols], pre[h][:, bank_cols], SIGMOID, bias=bias[:, i : i + 1])
+                if i == 0 and first == 0:
+                    nc.vector.tensor_tensor(value[:, cols], lin[h][:, bank_cols], gains[:, cols], MULT)
+                    nc.gpsimd.tensor_tensor(done[:, cols], sig[:, cols], value[:, cols], MULT)
+                    continue
                 nc.scalar.copy(value[:, cols], lin[h][:, bank_cols])
                 make_gate(i, cols)
                 if i > 0 or h == 0:
@@ -248,11 +265,11 @@ def tile_list_merge_conflict_scores_kernel(
         def fetch(dst, i, lst, first, count):
             nc.vector.tensor_copy(dst, pages[i][:].indirect(entries(lst, first, count)))
 
-        rows0_tile = shared.tile([P, M * PACK], BF16, offset=8192, align_bytes=64)
-        rows0 = rows0_tile[:].rearrange("p (b r) -> p b r", r=P * PACK)
-        first_pass_tile = shared.tile([P, M * PACK], BF16, offset=16384, align_bytes=64)
+        rows0_tile = shared.tile([P, M * PACK], BF16, offset=0, align_bytes=64)
+        rows0 = rows0_tile[:].rearrange("p (b u q e) -> p b u q e", u=2, q=P, e=2)
+        first_pass_tile = shared.tile([P, M * PACK], BF16, offset=8192, align_bytes=64)
         first_pass = first_pass_tile[:]
-        rows1 = [keep.tile([P, w // P, P * PACK], BF16, name="rows1_%d" % c) for c, w in enumerate(WIDTHS)]
+        rows1 = [keep.tile([P, w // P, 2, P, 2], BF16, name="rows1_%d" % c) for c, w in enumerate(WIDTHS)]
 
         theirs = {}
 
@@ -260,38 +277,47 @@ def tile_list_merge_conflict_scores_kernel(
             nc.vector.tensor_tensor(dst[:], pages[i][:].indirect(idx3[:]), theirs[i][:], SUBTRACT)
             excess = ring.tile([P, M], F32, name="excess", align_bytes=64)
             a, slot = divmod(i, TILES_PER_PASS)
-            r_cols = slice(slot * P, (slot + 1) * P)
+            q_cols = slice(slot * P // PACK, (slot + 1) * P // PACK)
             for h in range(M // BANK):
                 cols = slice(h * BANK, (h + 1) * BANK)
                 nc.scalar.activation(excess[:, cols], dst[:, cols], RELU)
             for h in range(M // BANK):
-                turned = psum.tile([P, BANK // P, P], F32, name="turn1")
+                turned = bank(4 + h, [P, BANK // P, P], F32, "sum")
                 for b in range(BANK // P):
                     cols = slice(h * BANK + b * P, h * BANK + (b + 1) * P)
                     nc.tensor.matmul(turned[:, b, :], theirs[i][:, cols], ident_f32[:], start=True, stop=False, is_transpose=True)
                     nc.tensor.matmul(turned[:, b, :], excess[:, cols], ident_f32[:], start=False, stop=True, is_transpose=True)
+                pairs = turned[:].rearrange("p b (q u e) -> p b u q e", u=2, e=2)
                 if a == 0:
-                    nc.scalar.copy(rows0[:, h * BANK // P : (h + 1) * BANK // P, r_cols], turned[:])
+                    nc.scalar.copy(rows0[:, h * BANK // P : (h + 1) * BANK // P, :, q_cols, :], pairs)
                 else:
                     for c in range(CHUNKS):
-                        if STARTS[c] // BANK == h:
-                            b0 = (STARTS[c] - h * BANK) // P
-                            nc.scalar.copy(rows1[c][:, :, r_cols], turned[:, b0 : b0 + WIDTHS[c] // P, :])
+                        lo, hi = max(STARTS[c], h * BANK), min(STARTS[c] + WIDTHS[c], (h + 1) * BANK)
+                        if lo < hi:
+                            nc.scalar.copy(
+                                rows1[c][:, (lo - STARTS[c]) // P : (hi - STARTS[c]) // P, :, q_cols, :],
+                                pairs[:, (lo - h * BANK) // P : (hi - h * BANK) // P],
+                            )
 
-        def turn_first(c, tiles, engine):
-            slot = TILES_PER_PASS - len(tiles)
+        def as_words(rows):
+            return rows.rearrange("p b u q e -> p b u (q e)").bitcast(F32)
+
+        def turn_first(c, z, engine):
             blocks = WIDTHS[c] // P
-            turned = psum.tile([P, blocks, len(tiles), P], BF16, name="turn1")
-            for e, z in enumerate(tiles):
-                for b in range(blocks):
-                    nc.tensor.transpose(turned[:, b, e, :], z[:, b * P : (b + 1) * P], ident_bf16[:])
-            move(engine, rows1[c][:, :, slot * P :], turned[:].rearrange("p b e r -> p b (e r)"))
+            turned = bank(5, [P, blocks, P], BF16, "first")
+            for b in range(blocks):
+                nc.tensor.transpose(turned[:, b, :], z[:, b * P : (b + 1) * P], ident_bf16[:])
+            move(
+                engine,
+                as_words(rows1[c][:])[:, :, :, P - P // PACK :],
+                turned[:].bitcast(F32).rearrange("p b (q u) -> p b u q", u=2),
+            )
 
-        def turn_second(words, blocks, grouped, engine):
-            turned = psum.tile([P, blocks, 2, P], F32, name="turn2")
+        def turn_second(step, words, blocks, grouped, engine):
+            turned = bank(6 + step % 2, [P, blocks, 2, P], F32, "second")
             for b in range(blocks):
                 for u in range(2):
-                    nc.tensor.transpose(turned[:, b, u, :], words[:, b, u : 2 * P : 2], ident_f32[:])
+                    nc.tensor.transpose(turned[:, b, u, :], words[:, b, u, :], ident_f32[:])
             move(
                 engine,
                 grouped.bitcast(F32).rearrange("p (b m u) -> p b m u", b=blocks, u=2),
@@ -309,33 +335,37 @@ def tile_list_merge_conflict_scores_kernel(
 
         sums = {}
 
+        def banks(c):
+            per_bank = BANK // WIDTHS[c]
+            return [range(t, t + per_bank) for t in range(0, N_TILES, per_bank)]
+
         def score_pass(a, c):
-            for pair in range(N_TILES // 2):
+            for g, tiles in enumerate(banks(c)):
                 if a == 0:
-                    sums[c, pair] = psum.tile([P, 2, WIDTHS[c]], F32, name="score", tag="acc", bufs=4)
-                for e in range(2):
-                    t = 2 * pair + e
+                    number = (N_TILES * STARTS[c] // BANK + g) % SCORE_BANKS
+                    sums[c, g] = bank(number, [P, len(tiles), WIDTHS[c]], F32, "score")
+                for e, t in enumerate(tiles):
                     nc.tensor.matmul_mx(
-                        out=sums[c, pair][:, e, :],
+                        out=sums[c, g][:, e, :],
                         lhsT=w8_codes[:, a, t * P : (t + 1) * P].bitcast(FP8X4),
                         lhsT_scale=w8_plane[:, a, t * P : (t + 1) * P],
                         rhs=z_codes[a][:, chunk(c)].bitcast(FP8X4),
                         rhs_scale=z_plane[a][:, chunk(c)],
                         start=(a == 0 and e == 0),
-                        stop=(a == PASSES - 1 and e == 1),
+                        stop=(a == PASSES - 1 and e == len(tiles) - 1),
                     )
 
         out_tiles = out.rearrange("(t p) m -> p t m", p=P)
-        staged = shared.tile([P, N_TILES * M], F32, offset=24576, align_bytes=64)
+        staged = shared.tile([P, N_TILES * M], F32, offset=16384, align_bytes=64)
 
         def store_scores(c):
-            for pair in range(N_TILES // 2):
-                first = N_TILES * STARTS[c] + pair * 2 * WIDTHS[c]
-                piece = staged[:, first : first + 2 * WIDTHS[c]].rearrange("p (e m) -> p e m", e=2)
-                move("vector" if c >= EARLY and pair == 1 else "scalar", piece, sums[c, pair][:])
-                nc.sync.dma_start(out_tiles[:, 2 * pair : 2 * pair + 2, chunk(c)], piece)
+            for g, tiles in enumerate(banks(c)):
+                first = N_TILES * STARTS[c] + g * BANK
+                piece = staged[:, first : first + BANK].rearrange("p (e m) -> p e m", e=len(tiles))
+                move("vector" if (c, g) in ON_VECTOR else "scalar", piece, sums[c, g][:])
+                nc.sync.dma_start(out_tiles[:, tiles.start : tiles.stop, chunk(c)], piece)
 
-        grouped0 = shared.tile([P, width * PACK], BF16, offset=4096, align_bytes=64)
+        grouped0 = keep.tile([P, width * PACK], BF16, align_bytes=64)
         quantize_wv(0, 1, grouped0[:])
         gather_second_pass()
         products(0, PIECE)
@@ -367,48 +397,46 @@ def tile_list_merge_conflict_scores_kernel(
                 quantize_wv(AHEAD, 2, values[i][:].bitcast(BF16))
             elif i + AHEAD < ROW_TILES:
                 quantize_wv(i + AHEAD, 1, values[i][:].bitcast(BF16))
-            if i == last - 1:
-                ours = keep.tile([P, M], BF16, align_bytes=64)
-                fetch(ours[:], i, idx3, 0, M)
-            else:
-                theirs[i] = wv_raw[i + AHEAD] if i + AHEAD < ROW_TILES else wv_raw[1]
-                fetch(theirs[i][:], i, idx4, 0, M)
+            theirs[i] = wv_raw[i + AHEAD] if i + AHEAD < ROW_TILES else wv_raw[i - TILES_PER_PASS]
+            fetch(theirs[i][:], i, idx4, 0, M)
             if i + LAG < ROW_TILES:
                 products(i + LAG, BANK)
             if i == TILES_PER_PASS - 1 + LAG:
-                words = rows0.bitcast(F32)
+                words = as_words(rows0)
                 for b in range(0, M // P, 2):
-                    turn_second(words[:, b : b + 2, :], 2, first_pass[:, PACK * P * b : PACK * P * (b + 2)], "scalar")
-        quantize_z(0, slice(0, M), first_pass)
+                    turn_second(b // 2, words[:, b : b + 2], 2, first_pass[:, PACK * P * b : PACK * P * (b + 2)], "scalar")
         difference(last - LAG, gates[last])
+        difference(last - 1, values[last])
         scatter(last, 0, S)
+        quantize_z(0, slice(0, M), first_pass)
+        for c in range(EARLY):
+            score_pass(0, c)
 
-        slot_cols = PACK * max(WIDTHS)
+        stage = [keep.tile([P, PACK * w], BF16, name="stage%d" % c, align_bytes=64) for c, w in enumerate(WIDTHS)]
         spent = placed[last][:].bitcast(BF16)
-        stage = [values[last][:, BANK:].bitcast(BF16), spent[:, :slot_cols], spent[:, slot_cols:]]
 
         def finish(c):
             if c >= EARLY:
                 score_pass(0, c)
-            quantize_z(1, chunk(c), stage[c % SLOTS][:, 0 : PACK * WIDTHS[c]])
+            quantize_z(1, chunk(c), stage[c][:])
             score_pass(1, c)
             store_scores(c)
 
-        for c in range(EARLY):
-            score_pass(0, c)
+        finished = 0
         for c in range(CHUNKS):
             w = WIDTHS[c]
-            if c >= SLOTS:
+            ours = spent[:, chunk(c)]
+            fetch(ours, last, idx3, STARTS[c], w)
+            other = spent[:, M + STARTS[c] : M + STARTS[c] + w]
+            if SLOTS <= c < PINNED:
                 finish(c - SLOTS)
-            slots = [stage[c % SLOTS][:, s * w : (s + 1) * w] for s in range(3)]
-            fetch(slots[0], last - 1, idx4, STARTS[c], w)
-            fetch(slots[1], last, idx3, STARTS[c], w)
-            fetch(slots[2], last, idx4, STARTS[c], w)
-            best = ring.tile([P, 2, w], BF16, name="best")
-            nc.vector.tensor_tensor(best[:, 0, :], ours[:, chunk(c)], slots[0], MAX)
-            nc.vector.tensor_tensor(best[:, 1, :], slots[1], slots[2], MAX)
+                finished = c - SLOTS + 1
+                other = stage[c - SLOTS][:, 0:w]
+            fetch(other, last, idx4, STARTS[c], w)
+            best = ring.tile([P, w], BF16, name="best", bufs=3)
+            nc.vector.tensor_tensor(best[:], ours, other, MAX)
             engine = "vector" if c == CHUNKS - 1 else "scalar"
-            turn_first(c, [best[:, 0, :], best[:, 1, :]], engine)
-            turn_second(rows1[c][:].bitcast(F32), w // P, stage[c % SLOTS][:, 0 : PACK * w], engine)
-        for c in range(CHUNKS - SLOTS, CHUNKS):
+            turn_first(c, best[:], engine)
+            turn_second(c, as_words(rows1[c][:]), w // P, stage[c][:], engine)
+        for c in range(finished, CHUNKS):
             finish(c)

@@ -26,7 +26,7 @@ PASSES = 2
 BANK = 512
 ROW_TILES = H // P
 TILES_PER_PASS = ROW_TILES // PASSES
-WIDTHS = [128, 256, 256, 256, 128]
+WIDTHS = [256, 256, 256, 128, 128]
 STARTS = [sum(WIDTHS[:c]) for c in range(len(WIDTHS))]
 CHUNKS = len(WIDTHS)
 N_TILES = N // P
@@ -34,11 +34,10 @@ LIST = 16
 W4_HEAD = 2
 AHEAD = 3
 LAG = 2
-EARLY = 3
+EARLY = 2
 SCORE_BANKS = 5
-SLOTS = 2
-PINNED = 0
-ON_VECTOR = [(2, 1), (3, 1), (4, 0)]
+SLOTS = 3
+ON_VECTOR = [(2, 1), (4, 0)]
 PIECE = 256
 
 
@@ -82,22 +81,15 @@ def tile_list_merge_conflict_scores_kernel(
             else:
                 nc.scalar.copy(dst, src)
 
-        tab_plane = [keep.tile([P, T], U8, name="tab_plane%d" % a, align_bytes=64) for a in range(PASSES)]
-        for a in range(PASSES):
-            nc.vector.memset(tab_plane[a][:].bitcast(I32), 0)
-
-        def load_tab_plane(a):
-            for q in range(4):
-                nc.sync.dma_start(
-                    tab_plane[a][:].bitcast(I32)[32 * q : 32 * q + 4, :], tab_scales.bitcast(I32)[a, 4 * q : 4 * q + 4, :]
-                )
-
+        tab_plane = keep.tile([P, T], U8, align_bytes=64)
+        nc.vector.memset(tab_plane[:].bitcast(I32), 0)
         w4_plane = keep.tile([P, PASSES, H], U8, align_bytes=64)
-        nc.gpsimd.memset(w4_plane[:].rearrange("p a c -> p (a c)").bitcast(I32), 0)
-        load_plane(nc.gpsimd, w4_plane, w4_scales)
+        zero_plane(w4_plane)
         bg_rows = keep.tile([P, P], F32)
-        nc.vector.memset(bg_rows[:], 0.0)
+        nc.gpsimd.memset(bg_rows[:], 0.0)
+        nc.gpsimd.dma_start(bg_rows[0:ROW_TILES, :], bg.rearrange("(i p) -> i p", p=P))
         v_plane = [keep.tile([P, S], U8, name="v_plane%d" % a, align_bytes=64) for a in range(PASSES)]
+        nc.vector.memset(v_plane[1][:].bitcast(I32), 0)
         w8_plane = keep.tile([P, PASSES, N], U8, align_bytes=64)
         zero_plane(w8_plane)
         ident_f32 = keep.tile([P, P], F32)
@@ -115,7 +107,10 @@ def tile_list_merge_conflict_scores_kernel(
                 return w4_head[:, a, 2 * P * i : 2 * P * (i + 1)]
             return w4_rest[:, a, 2 * P * (i - W4_HEAD) : 2 * P * (i - W4_HEAD + 1)]
 
-        wv_raw = [keep.tile([P, PASSES * PACK * P], F32, name="wv_raw%d" % i, align_bytes=64) for i in range(ROW_TILES)]
+        wv_raw = [
+            shared.tile([P, PASSES * PACK * P], F32, name="wv_raw%d" % i, offset=32768 + 4096 * i, align_bytes=64)
+            for i in range(ROW_TILES)
+        ]
         pages = {}
 
         def raw_pass(i, a):
@@ -137,27 +132,28 @@ def tile_list_merge_conflict_scores_kernel(
         tab = [shared.tile([P, T], I32, name="tab%d" % a, offset=16384 * a, align_bytes=64) for a in range(PASSES)]
         tab_src = [tab_words[a].rearrange("p t i -> p (t i)").bitcast(I32) for a in range(PASSES)]
         nc.sync.dma_start(tab[0][:, : T // 4], tab_src[0][:, : T // 4])
-        load_tab_plane(0)
+        rows = tab_scales.bitcast(I32).rearrange("a (q r) c -> r q a c", r=4)
+        for r in range(4):
+            nc.sync.dma_start(tab_plane[:].bitcast(I32)[r:P:16, :], rows[r])
         idx = load_list(offs, "idx")
-        nc.sync.dma_start(tab[0][:, T // 4 :], tab_src[0][:, T // 4 :])
+        for cols in (slice(T // 4, 5 * T // 8), slice(5 * T // 8, T)):
+            nc.sync.dma_start(tab[0][:, cols], tab_src[0][:, cols])
         nc.sync.dma_start(w4_head[:].bitcast(I32), w4_src[:, :, 0:head_words])
+        load_plane(nc.sync, w4_plane, w4_scales)
         load_wv(0)
-        load_tab_plane(1)
-        nc.sync.dma_start(bg_rows[0:ROW_TILES, :], bg.rearrange("(i p) -> i p", p=P))
         for h in range(2):
             nc.sync.dma_start(tab[1][:, h * T // 2 : (h + 1) * T // 2], tab_src[1][:, h * T // 2 : (h + 1) * T // 2])
         idx2 = load_list(offs2, "idx2")
+        idx3 = load_list(offs3, "idx3")
+        idx4 = load_list(offs4, "idx4")
         gains = keep.tile([P, S], F32)
         nc.sync.dma_start(gains[:, :BANK], wgs[:, :BANK])
-        load_wv_pass(1, 0)
         load_page(0)
-        load_wv_pass(1, 1)
         nc.sync.dma_start(gains[:, BANK:], wgs[:, BANK:])
+        load_wv(1)
         load_wv(2)
         load_page(1)
         nc.sync.dma_start(w4_rest[:].bitcast(I32), w4_src[:, :, head_words:])
-        idx3 = load_list(offs3, "idx3")
-        idx4 = load_list(offs4, "idx4")
         load_wv(3)
         load_wv(4)
         load_page(2)
@@ -176,9 +172,9 @@ def tile_list_merge_conflict_scores_kernel(
         nc.scalar.copy(bias[:], bg_turned[:, 0:ROW_TILES])
 
         v_codes = [keep.tile([P, S], U32, name="v_codes%d" % a, align_bytes=64) for a in range(PASSES)]
-        nc.vector.tensor_copy(v_plane[0][:], tab_plane[0][:].indirect(idx[:]))
+        nc.vector.tensor_copy(v_plane[0][:], tab_plane[:].indirect(idx[:]))
+        nc.gpsimd.dma_start(v_plane[1][:].bitcast(I32)[0:100, :], v_plane[0][:].bitcast(I32)[16:116, :])
         nc.vector.tensor_copy(v_codes[0][:], tab[0][:].bitcast(U32).indirect(idx[:]))
-        nc.vector.tensor_copy(v_plane[1][:], tab_plane[1][:].indirect(idx[:]))
 
         def gather_second_pass():
             for h in range(S // BANK):
@@ -216,7 +212,7 @@ def tile_list_merge_conflict_scores_kernel(
             sig = ring.tile([P, S], F32, name="sig", align_bytes=64)
             gate = ring.tile([P, S], F32, name="gate", align_bytes=64)
             value = ring.tile([P, S], F32, name="value", bufs=3, align_bytes=64)
-            done = ring.tile([P, S], F32, name="placed", align_bytes=64)
+            done = ring.tile([P, S], F32, name="placed", bufs=3, align_bytes=64)
             halves = [slice(h * BANK, (h + 1) * BANK) for h in range(S // BANK)]
             pre = [bank(2 * h, [P, BANK], F32, "pre") for h in range(len(halves))]
             lin = [bank(2 * h + 1, [P, BANK], F32, "lin") for h in range(len(halves))]
@@ -233,9 +229,12 @@ def tile_list_merge_conflict_scores_kernel(
                 )
 
             def both(a, h):
-                one_pass(pre[h], w4_codes(a, i).bitcast(FP4X4), w4_plane[:, a, i * P : (i + 1) * P], a, halves[h])
                 cols = slice(i * width + a * P, i * width + (a + 1) * P)
-                one_pass(lin[h], wv_codes[:, cols].bitcast(FP8X4), wv_plane[:, cols], a, halves[h])
+                if i == 0 and h == 0:
+                    one_pass(lin[h], wv_codes[:, cols].bitcast(FP8X4), wv_plane[:, cols], a, halves[h])
+                one_pass(pre[h], w4_codes(a, i).bitcast(FP4X4), w4_plane[:, a, i * P : (i + 1) * P], a, halves[h])
+                if i > 0 or h > 0:
+                    one_pass(lin[h], wv_codes[:, cols].bitcast(FP8X4), wv_plane[:, cols], a, halves[h])
 
             order = [(a, h) for h in range(len(halves)) for a in range(PASSES)]
             if i == 0:
@@ -247,7 +246,7 @@ def tile_list_merge_conflict_scores_kernel(
                 h, local = divmod(first, BANK)
                 cols, bank_cols = slice(first, first + piece), slice(local, local + piece)
                 nc.scalar.activation(sig[:, cols], pre[h][:, bank_cols], SIGMOID, bias=bias[:, i : i + 1])
-                if i == 0 and first == 0:
+                if i == 0 and h == 0:
                     nc.vector.tensor_tensor(value[:, cols], lin[h][:, bank_cols], gains[:, cols], MULT)
                     nc.gpsimd.tensor_tensor(done[:, cols], sig[:, cols], value[:, cols], MULT)
                     continue
@@ -269,52 +268,59 @@ def tile_list_merge_conflict_scores_kernel(
         rows0 = rows0_tile[:].rearrange("p (b u q e) -> p b u q e", u=2, q=P, e=2)
         first_pass_tile = shared.tile([P, M * PACK], BF16, offset=8192, align_bytes=64)
         first_pass = first_pass_tile[:]
-        rows1 = [keep.tile([P, w // P, 2, P, 2], BF16, name="rows1_%d" % c) for c, w in enumerate(WIDTHS)]
+        rows1_tile = keep.tile([P, M * PACK], BF16, align_bytes=64)
+        rows1 = rows1_tile[:].rearrange("p (b u q e) -> p b u q e", u=2, q=P, e=2)
 
-        theirs = {}
+        def rows_of(c):
+            return rows1[:, STARTS[c] // P : (STARTS[c] + WIDTHS[c]) // P]
+
+
+        theirs, excesses = {}, {}
 
         def difference(i, dst):
             nc.vector.tensor_tensor(dst[:], pages[i][:].indirect(idx3[:]), theirs[i][:], SUBTRACT)
-            excess = ring.tile([P, M], F32, name="excess", align_bytes=64)
+            if i == TILES_PER_PASS:
+                excess = rows0_tile[:].bitcast(F32)[:, 0:M]
+            else:
+                excess = ring.tile([P, M], F32, name="excess", align_bytes=64)
+            excesses[i] = excess
             a, slot = divmod(i, TILES_PER_PASS)
             q_cols = slice(slot * P // PACK, (slot + 1) * P // PACK)
             for h in range(M // BANK):
                 cols = slice(h * BANK, (h + 1) * BANK)
                 nc.scalar.activation(excess[:, cols], dst[:, cols], RELU)
             for h in range(M // BANK):
-                turned = bank(4 + h, [P, BANK // P, P], F32, "sum")
-                for b in range(BANK // P):
-                    cols = slice(h * BANK + b * P, h * BANK + (b + 1) * P)
-                    nc.tensor.matmul(turned[:, b, :], theirs[i][:, cols], ident_f32[:], start=True, stop=False, is_transpose=True)
-                    nc.tensor.matmul(turned[:, b, :], excess[:, cols], ident_f32[:], start=False, stop=True, is_transpose=True)
+                turned = bank({5: 0}.get(i, 4) + h, [P, BANK // P, P], F32, "sum")
+                for term, src in enumerate((theirs[i], excess)):
+                    for b in range(BANK // P):
+                        nc.tensor.matmul(
+                            turned[:, b, :],
+                            src[:, h * BANK + b * P : h * BANK + (b + 1) * P],
+                            ident_f32[:],
+                            start=(term == 0 and b == 0),
+                            stop=(term == 1 and b == BANK // P - 1),
+                            is_transpose=True,
+                        )
                 pairs = turned[:].rearrange("p b (q u e) -> p b u q e", u=2, e=2)
-                if a == 0:
-                    nc.scalar.copy(rows0[:, h * BANK // P : (h + 1) * BANK // P, :, q_cols, :], pairs)
-                else:
-                    for c in range(CHUNKS):
-                        lo, hi = max(STARTS[c], h * BANK), min(STARTS[c] + WIDTHS[c], (h + 1) * BANK)
-                        if lo < hi:
-                            nc.scalar.copy(
-                                rows1[c][:, (lo - STARTS[c]) // P : (hi - STARTS[c]) // P, :, q_cols, :],
-                                pairs[:, (lo - h * BANK) // P : (hi - h * BANK) // P],
-                            )
+                nc.scalar.copy((rows0, rows1)[a][:, h * BANK // P : (h + 1) * BANK // P, :, q_cols, :], pairs)
 
         def as_words(rows):
             return rows.rearrange("p b u q e -> p b u (q e)").bitcast(F32)
 
-        def turn_first(c, z, engine):
+        def turn_first(c, best, engine):
             blocks = WIDTHS[c] // P
-            turned = bank(5, [P, blocks, P], BF16, "first")
-            for b in range(blocks):
-                nc.tensor.transpose(turned[:, b, :], z[:, b * P : (b + 1) * P], ident_bf16[:])
+            turned = bank(5, [P, blocks, 2, P], BF16, "first")
+            for e in range(2):
+                for b in range(blocks):
+                    nc.tensor.transpose(turned[:, b, e, :], best[:, e, b * P : (b + 1) * P], ident_bf16[:])
             move(
                 engine,
-                as_words(rows1[c][:])[:, :, :, P - P // PACK :],
-                turned[:].bitcast(F32).rearrange("p b (q u) -> p b u q", u=2),
+                as_words(rows_of(c))[:, :, :, P // 2 :],
+                turned[:].rearrange("p b e r -> p b (e r)").bitcast(F32).rearrange("p b (q u) -> p b u q", u=2),
             )
 
-        def turn_second(step, words, blocks, grouped, engine):
-            turned = bank(6 + step % 2, [P, blocks, 2, P], F32, "second")
+        def turn_second(number, words, blocks, grouped, engine):
+            turned = bank(number, [P, blocks, 2, P], F32, "second")
             for b in range(blocks):
                 for u in range(2):
                     nc.tensor.transpose(turned[:, b, u, :], words[:, b, u, :], ident_f32[:])
@@ -397,46 +403,48 @@ def tile_list_merge_conflict_scores_kernel(
                 quantize_wv(AHEAD, 2, values[i][:].bitcast(BF16))
             elif i + AHEAD < ROW_TILES:
                 quantize_wv(i + AHEAD, 1, values[i][:].bitcast(BF16))
-            theirs[i] = wv_raw[i + AHEAD] if i + AHEAD < ROW_TILES else wv_raw[i - TILES_PER_PASS]
-            fetch(theirs[i][:], i, idx4, 0, M)
+            if i == last - 1:
+                ours = keep.tile([P, M], BF16, align_bytes=64)
+                fetch(ours[:], i, idx3, 0, M)
+            else:
+                theirs[i] = wv_raw[i + AHEAD] if i + AHEAD < ROW_TILES else wv_raw[1]
+                fetch(theirs[i][:], i, idx4, 0, M)
             if i + LAG < ROW_TILES:
                 products(i + LAG, BANK)
             if i == TILES_PER_PASS - 1 + LAG:
                 words = as_words(rows0)
                 for b in range(0, M // P, 2):
                     turn_second(b // 2, words[:, b : b + 2], 2, first_pass[:, PACK * P * b : PACK * P * (b + 2)], "scalar")
-        difference(last - LAG, gates[last])
-        difference(last - 1, values[last])
-        scatter(last, 0, S)
         quantize_z(0, slice(0, M), first_pass)
+        difference(last - LAG, gates[last])
+        scatter(last, 0, S)
         for c in range(EARLY):
             score_pass(0, c)
 
-        stage = [keep.tile([P, PACK * w], BF16, name="stage%d" % c, align_bytes=64) for c, w in enumerate(WIDTHS)]
+        slot_cols = PACK * max(WIDTHS)
         spent = placed[last][:].bitcast(BF16)
+        stage = [values[last][:, BANK:].bitcast(BF16), spent[:, :slot_cols], spent[:, slot_cols:]]
 
         def finish(c):
             if c >= EARLY:
                 score_pass(0, c)
-            quantize_z(1, chunk(c), stage[c][:])
+            quantize_z(1, chunk(c), stage[c % SLOTS][:, 0 : PACK * WIDTHS[c]])
             score_pass(1, c)
             store_scores(c)
 
-        finished = 0
         for c in range(CHUNKS):
             w = WIDTHS[c]
-            ours = spent[:, chunk(c)]
-            fetch(ours, last, idx3, STARTS[c], w)
-            other = spent[:, M + STARTS[c] : M + STARTS[c] + w]
-            if SLOTS <= c < PINNED:
+            if c >= SLOTS:
                 finish(c - SLOTS)
-                finished = c - SLOTS + 1
-                other = stage[c - SLOTS][:, 0:w]
-            fetch(other, last, idx4, STARTS[c], w)
-            best = ring.tile([P, w], BF16, name="best", bufs=3)
-            nc.vector.tensor_tensor(best[:], ours, other, MAX)
+            slots = [stage[c % SLOTS][:, s * w : (s + 1) * w] for s in range(3)]
+            fetch(slots[0], last - 1, idx4, STARTS[c], w)
+            fetch(slots[1], last, idx3, STARTS[c], w)
+            fetch(slots[2], last, idx4, STARTS[c], w)
+            best = ring.tile([P, 2, w], BF16, name="best")
+            nc.vector.tensor_tensor(best[:, 0, :], ours[:, chunk(c)], slots[0], MAX)
+            nc.vector.tensor_tensor(best[:, 1, :], slots[1], slots[2], MAX)
             engine = "vector" if c == CHUNKS - 1 else "scalar"
-            turn_first(c, best[:], engine)
-            turn_second(c, as_words(rows1[c][:]), w // P, stage[c][:], engine)
-        for c in range(finished, CHUNKS):
+            turn_first(c, best, engine)
+            turn_second(6 + c % 2, as_words(rows_of(c)), w // P, stage[c % SLOTS][:, 0 : PACK * w], engine)
+        for c in range(CHUNKS - SLOTS, CHUNKS):
             finish(c)

@@ -37,7 +37,7 @@ LAG = 2
 EARLY = 2
 SCORE_BANKS = 5
 SLOTS = 3
-ON_VECTOR = [(2, 1), (4, 0)]
+ON_VECTOR = [(2, 1), (4, 1)]
 PIECE = 256
 
 
@@ -200,7 +200,7 @@ def tile_list_merge_conflict_scores_kernel(
                 out=wv_codes[:, cols].bitcast(FP8X4), scales=wv_plane[:, cols], in_=grouped[:, 0 : count * width * PACK]
             )
 
-        sigs, gates, values, placed = {}, {}, {}, {}
+        sigs, gates, values, placed, theirs = {}, {}, {}, {}, {}
 
         def make_gate(i, cols):
             nc.gpsimd.tensor_tensor(gates[i][:, cols], sigs[i][:, cols], gains[:, cols], MULT)
@@ -210,9 +210,10 @@ def tile_list_merge_conflict_scores_kernel(
 
         def products(i, piece):
             sig = ring.tile([P, S], F32, name="sig", align_bytes=64)
-            gate = ring.tile([P, S], F32, name="gate", align_bytes=64)
             value = ring.tile([P, S], F32, name="value", bufs=3, align_bytes=64)
-            done = ring.tile([P, S], F32, name="placed", bufs=3, align_bytes=64)
+            if i < AHEAD:
+                gates[i] = ring.tile([P, S], F32, name="gate%d" % (i // 2), bufs=1, align_bytes=64)
+                placed[i] = done = ring.tile([P, S], F32, name="placed", align_bytes=64)
             halves = [slice(h * BANK, (h + 1) * BANK) for h in range(S // BANK)]
             pre = [bank(2 * h, [P, BANK], F32, "pre") for h in range(len(halves))]
             lin = [bank(2 * h + 1, [P, BANK], F32, "lin") for h in range(len(halves))]
@@ -241,7 +242,7 @@ def tile_list_merge_conflict_scores_kernel(
                 order = [(a, h) for a in range(PASSES) for h in range(len(halves))]
             for a, h in order:
                 both(a, h)
-            sigs[i], gates[i], values[i], placed[i] = sig, gate, value, done
+            sigs[i], values[i] = sig, value
             for first in range(0, S, piece):
                 h, local = divmod(first, BANK)
                 cols, bank_cols = slice(first, first + piece), slice(local, local + piece)
@@ -251,9 +252,18 @@ def tile_list_merge_conflict_scores_kernel(
                     nc.gpsimd.tensor_tensor(done[:, cols], sig[:, cols], value[:, cols], MULT)
                     continue
                 nc.scalar.copy(value[:, cols], lin[h][:, bank_cols])
-                make_gate(i, cols)
-                if i > 0 or h == 0:
+                if i < AHEAD:
+                    make_gate(i, cols)
+                if 0 < i < AHEAD:
                     make_placed(i, cols, done[:, cols])
+
+        def combine(i):
+            gates[i] = theirs[i - AHEAD]
+            placed[i] = ring.tile([P, S], F32, name="placed", align_bytes=64)
+            for first in range(0, S, BANK):
+                cols = slice(first, first + BANK)
+                make_gate(i, cols)
+                make_placed(i, cols, placed[i][:, cols])
 
         def scatter_from(i, first, count, src):
             nc.vector.tensor_copy(pages[i][:].indirect(entries(idx2, first, count)), src)
@@ -275,7 +285,7 @@ def tile_list_merge_conflict_scores_kernel(
             return rows1[:, STARTS[c] // P : (STARTS[c] + WIDTHS[c]) // P]
 
 
-        theirs, excesses = {}, {}
+        excesses = {}
 
         def difference(i, dst):
             nc.vector.tensor_tensor(dst[:], pages[i][:].indirect(idx3[:]), theirs[i][:], SUBTRACT)
@@ -330,7 +340,7 @@ def tile_list_merge_conflict_scores_kernel(
                 turned[:].rearrange("p b u m -> p b m u"),
             )
 
-        z_codes = [keep.tile([P, M], U32, name="z_codes%d" % a, align_bytes=64) for a in range(PASSES)]
+        z_codes = {1: keep.tile([P, M], U32, name="z_codes", align_bytes=64)}
         z_plane = [keep.tile([P, M], U8, name="z_plane%d" % a, align_bytes=64) for a in range(PASSES)]
 
         def chunk(c):
@@ -342,7 +352,7 @@ def tile_list_merge_conflict_scores_kernel(
         sums = {}
 
         def banks(c):
-            per_bank = BANK // WIDTHS[c]
+            per_bank = 2 if c == CHUNKS - 1 else BANK // WIDTHS[c]
             return [range(t, t + per_bank) for t in range(0, N_TILES, per_bank)]
 
         def score_pass(a, c):
@@ -366,8 +376,8 @@ def tile_list_merge_conflict_scores_kernel(
 
         def store_scores(c):
             for g, tiles in enumerate(banks(c)):
-                first = N_TILES * STARTS[c] + g * BANK
-                piece = staged[:, first : first + BANK].rearrange("p (e m) -> p e m", e=len(tiles))
+                first = N_TILES * STARTS[c] + tiles.start * WIDTHS[c]
+                piece = staged[:, first : first + len(tiles) * WIDTHS[c]].rearrange("p (e m) -> p e m", e=len(tiles))
                 move("vector" if (c, g) in ON_VECTOR else "scalar", piece, sums[c, g][:])
                 nc.sync.dma_start(out_tiles[:, tiles.start : tiles.stop, chunk(c)], piece)
 
@@ -389,41 +399,39 @@ def tile_list_merge_conflict_scores_kernel(
         products(2, BANK)
 
         last = ROW_TILES - 1
-        for i in range(1, last):
+        for i in range(1, last - 1):
             if i == 1:
                 for first in range(0, S, BANK):
                     scatter(i, first, BANK)
             else:
-                scatter(i, 0, S)
-            if i >= LAG:
                 difference(i - LAG, gates[i])
+                combine(i + 1)
                 if i + AHEAD < ROW_TILES:
                     load_page(i + AHEAD)
-            if i == 1:
-                quantize_wv(AHEAD, 2, values[i][:].bitcast(BF16))
-            elif i + AHEAD < ROW_TILES:
-                quantize_wv(i + AHEAD, 1, values[i][:].bitcast(BF16))
-            if i == last - 1:
-                ours = keep.tile([P, M], BF16, align_bytes=64)
-                fetch(ours[:], i, idx3, 0, M)
-            else:
-                theirs[i] = wv_raw[i + AHEAD] if i + AHEAD < ROW_TILES else wv_raw[1]
+                scatter(i, 0, S)
+            if i + AHEAD < ROW_TILES:
+                quantize_wv(AHEAD if i == 1 else i + AHEAD, 2 if i == 1 else 1, values[i][:].bitcast(BF16))
+                theirs[i] = wv_raw[i + AHEAD]
                 fetch(theirs[i][:], i, idx4, 0, M)
-            if i + LAG < ROW_TILES:
-                products(i + LAG, BANK)
-            if i == TILES_PER_PASS - 1 + LAG:
-                words = as_words(rows0)
-                for b in range(0, M // P, 2):
-                    turn_second(b // 2, words[:, b : b + 2], 2, first_pass[:, PACK * P * b : PACK * P * (b + 2)], "scalar")
-        quantize_z(0, slice(0, M), first_pass)
-        difference(last - LAG, gates[last])
+            products(i + LAG, BANK)
+        words = as_words(rows0)
+        for b in range(0, M // P, 2):
+            turn_second(b // 2, words[:, b : b + 2], 2, first_pass[:, PACK * P * b : PACK * P * (b + 2)], "scalar")
+
+        difference(last - 3, gates[last - 1])
+        combine(last)
+        theirs[last - 2] = values[last - 1]
+        fetch(theirs[last - 2][:], last - 2, idx4, 0, M)
+        scatter(last - 1, 0, S)
+        difference(last - 2, gates[last])
+        ours = values[last][:, :BANK].bitcast(BF16)
+        fetch(ours, last - 1, idx3, 0, M)
         scatter(last, 0, S)
-        for c in range(EARLY):
-            score_pass(0, c)
 
         slot_cols = PACK * max(WIDTHS)
-        spent = placed[last][:].bitcast(BF16)
+        spent = ring.tile([P, 2 * slot_cols], BF16, name="placed", align_bytes=64)
         stage = [values[last][:, BANK:].bitcast(BF16), spent[:, :slot_cols], spent[:, slot_cols:]]
+        z_codes[0] = ring.tile([P, M], U32, name="placed", align_bytes=64)
 
         def finish(c):
             if c >= EARLY:
@@ -438,6 +446,10 @@ def tile_list_merge_conflict_scores_kernel(
                 finish(c - SLOTS)
             slots = [stage[c % SLOTS][:, s * w : (s + 1) * w] for s in range(3)]
             fetch(slots[0], last - 1, idx4, STARTS[c], w)
+            if c == 0:
+                quantize_z(0, slice(0, M), first_pass)
+                for early in range(EARLY):
+                    score_pass(0, early)
             fetch(slots[1], last, idx3, STARTS[c], w)
             fetch(slots[2], last, idx4, STARTS[c], w)
             best = ring.tile([P, 2, w], BF16, name="best")

@@ -31,13 +31,13 @@ STARTS = [sum(WIDTHS[:c]) for c in range(len(WIDTHS))]
 CHUNKS = len(WIDTHS)
 N_TILES = N // P
 LIST = 16
-W4_HEAD = 2
+W4_HEAD = 3
 AHEAD = 3
 LAG = 2
 EARLY = 2
 SCORE_BANKS = 5
 SLOTS = 3
-ON_VECTOR = [(2, 1), (4, 1)]
+ON_VECTOR = [(2, 1), (3, 0), (4, 1)]
 PIECE = 256
 
 
@@ -83,8 +83,16 @@ def tile_list_merge_conflict_scores_kernel(
 
         tab_plane = keep.tile([P, T], U8, align_bytes=64)
         nc.vector.memset(tab_plane[:].bitcast(I32), 0)
-        w4_plane = keep.tile([P, PASSES, H], U8, align_bytes=64)
-        zero_plane(w4_plane)
+        head_cols = W4_HEAD * P
+        w4_plane = [keep.tile([P, PASSES, w], U8, name="w4_plane%d" % w, align_bytes=64) for w in (head_cols, H - head_cols)]
+        for plane in w4_plane:
+            zero_plane(plane)
+
+        def w4_scale(a, i):
+            if i < W4_HEAD:
+                return w4_plane[0][:, a, i * P : (i + 1) * P]
+            return w4_plane[1][:, a, (i - W4_HEAD) * P : (i - W4_HEAD + 1) * P]
+
         bg_rows = keep.tile([P, P], F32)
         nc.gpsimd.memset(bg_rows[:], 0.0)
         nc.gpsimd.dma_start(bg_rows[0:ROW_TILES, :], bg.rearrange("(i p) -> i p", p=P))
@@ -139,7 +147,7 @@ def tile_list_merge_conflict_scores_kernel(
         for cols in (slice(T // 4, 5 * T // 8), slice(5 * T // 8, T)):
             nc.sync.dma_start(tab[0][:, cols], tab_src[0][:, cols])
         nc.sync.dma_start(w4_head[:].bitcast(I32), w4_src[:, :, 0:head_words])
-        load_plane(nc.sync, w4_plane, w4_scales)
+        load_plane(nc.sync, w4_plane[0], w4_scales[:, :, :head_cols])
         load_wv(0)
         for h in range(2):
             nc.sync.dma_start(tab[1][:, h * T // 2 : (h + 1) * T // 2], tab_src[1][:, h * T // 2 : (h + 1) * T // 2])
@@ -154,6 +162,7 @@ def tile_list_merge_conflict_scores_kernel(
         load_wv(2)
         load_page(1)
         nc.sync.dma_start(w4_rest[:].bitcast(I32), w4_src[:, :, head_words:])
+        load_plane(nc.sync, w4_plane[1], w4_scales[:, :, head_cols:])
         load_wv(3)
         load_wv(4)
         load_page(2)
@@ -168,8 +177,13 @@ def tile_list_merge_conflict_scores_kernel(
 
         bg_turned = bank(7, [P, P], F32, "bias")
         nc.tensor.transpose(bg_turned[:], bg_rows[:], ident_f32[:])
-        bias = keep.tile([P, ROW_TILES], F32)
-        nc.scalar.copy(bias[:], bg_turned[:, 0:ROW_TILES])
+        bias_first = keep.tile([P, 1], F32)
+        nc.scalar.copy(bias_first[:], bg_turned[:, 0:1])
+
+        def bias(i):
+            if i == 0:
+                return bias_first[:]
+            return wv_raw[1][:, S - ROW_TILES + i : S - ROW_TILES + i + 1]
 
         v_codes = [keep.tile([P, S], U32, name="v_codes%d" % a, align_bytes=64) for a in range(PASSES)]
         nc.vector.tensor_copy(v_plane[0][:], tab_plane[:].indirect(idx[:]))
@@ -209,53 +223,54 @@ def tile_list_merge_conflict_scores_kernel(
             nc.gpsimd.tensor_tensor(dst, gates[i][:, cols], values[i][:, cols], MULT)
 
         def products(i, piece):
-            sig = ring.tile([P, S], F32, name="sig", align_bytes=64)
+            sigs[i] = sig = ring.tile([P, S], F32, name="sig", align_bytes=64)
             value = ring.tile([P, S], F32, name="value", bufs=3, align_bytes=64)
             if i < AHEAD:
-                gates[i] = ring.tile([P, S], F32, name="gate%d" % (i // 2), bufs=1, align_bytes=64)
+                gates[i] = ring.tile([P, S], F32, name="gate", bufs=1, align_bytes=64)
                 placed[i] = done = ring.tile([P, S], F32, name="placed", align_bytes=64)
-            halves = [slice(h * BANK, (h + 1) * BANK) for h in range(S // BANK)]
-            pre = [bank(2 * h, [P, BANK], F32, "pre") for h in range(len(halves))]
-            lin = [bank(2 * h + 1, [P, BANK], F32, "lin") for h in range(len(halves))]
+            values[i] = value
+            spans = [(0, PIECE), (PIECE, PIECE), (BANK, BANK)] if i == 0 else [(0, BANK), (BANK, BANK)]
+            numbers = [0, 4, 2] if i == 0 else [0, 2]
+            pre = [bank(n + i % 2, [P, count], F32, "pre") for n, (first, count) in zip(numbers, spans)]
+            lin = [bank(n + (i + 1) % 2, [P, count], F32, "lin") for n, (first, count) in zip(numbers, spans)]
 
-            def one_pass(acc, codes, plane, a, cols):
-                nc.tensor.matmul_mx(
-                    out=acc[:],
-                    lhsT=codes,
-                    lhsT_scale=plane,
-                    rhs=v_codes[a][:, cols].bitcast(FP8X4),
-                    rhs_scale=v_plane[a][:, cols],
-                    start=(a == 0),
-                    stop=(a == PASSES - 1),
-                )
+            def one_pass(acc, codes, plane, a, first, count, step):
+                for local in range(0, count, step):
+                    cols = slice(first + local, first + local + step)
+                    nc.tensor.matmul_mx(
+                        out=acc[:, local : local + step],
+                        lhsT=codes,
+                        lhsT_scale=plane,
+                        rhs=v_codes[a][:, cols].bitcast(FP8X4),
+                        rhs_scale=v_plane[a][:, cols],
+                        start=(a == 0 and local == 0),
+                        stop=(a == PASSES - 1 and local + step == count),
+                    )
 
-            def both(a, h):
+            def both(a, g):
+                first, count = spans[g]
                 cols = slice(i * width + a * P, i * width + (a + 1) * P)
-                if i == 0 and h == 0:
-                    one_pass(lin[h], wv_codes[:, cols].bitcast(FP8X4), wv_plane[:, cols], a, halves[h])
-                one_pass(pre[h], w4_codes(a, i).bitcast(FP4X4), w4_plane[:, a, i * P : (i + 1) * P], a, halves[h])
-                if i > 0 or h > 0:
-                    one_pass(lin[h], wv_codes[:, cols].bitcast(FP8X4), wv_plane[:, cols], a, halves[h])
+                one_pass(pre[g], w4_codes(a, i).bitcast(FP4X4), w4_scale(a, i), a, first, count, BANK if count == BANK else P)
+                one_pass(lin[g], wv_codes[:, cols].bitcast(FP8X4), wv_plane[:, cols], a, first, count, count)
 
-            order = [(a, h) for h in range(len(halves)) for a in range(PASSES)]
+            order = [(a, g) for g in range(len(spans)) for a in range(PASSES)]
             if i == 0:
-                order = [(a, h) for a in range(PASSES) for h in range(len(halves))]
-            for a, h in order:
-                both(a, h)
-            sigs[i], values[i] = sig, value
-            for first in range(0, S, piece):
-                h, local = divmod(first, BANK)
-                cols, bank_cols = slice(first, first + piece), slice(local, local + piece)
-                nc.scalar.activation(sig[:, cols], pre[h][:, bank_cols], SIGMOID, bias=bias[:, i : i + 1])
-                if i == 0 and h == 0:
-                    nc.vector.tensor_tensor(value[:, cols], lin[h][:, bank_cols], gains[:, cols], MULT)
-                    nc.gpsimd.tensor_tensor(done[:, cols], sig[:, cols], value[:, cols], MULT)
-                    continue
-                nc.scalar.copy(value[:, cols], lin[h][:, bank_cols])
-                if i < AHEAD:
-                    make_gate(i, cols)
-                if 0 < i < AHEAD:
-                    make_placed(i, cols, done[:, cols])
+                order = [(a, g) for a in range(PASSES) for g in range(len(spans))]
+            for a, g in order:
+                both(a, g)
+            for g, (start, count) in enumerate(spans):
+                for local in range(0, count, piece):
+                    cols, bank_cols = slice(start + local, start + local + piece), slice(local, local + piece)
+                    nc.scalar.activation(sig[:, cols], pre[g][:, bank_cols], SIGMOID, bias=bias(i))
+                    if count == PIECE:
+                        nc.vector.tensor_tensor(value[:, cols], lin[g][:, bank_cols], gains[:, cols], MULT)
+                        nc.gpsimd.tensor_tensor(done[:, cols], sig[:, cols], value[:, cols], MULT)
+                        continue
+                    nc.scalar.copy(value[:, cols], lin[g][:, bank_cols])
+                    if i < AHEAD:
+                        make_gate(i, cols)
+                    if 0 < i < AHEAD:
+                        make_placed(i, cols, done[:, cols])
 
         def combine(i):
             gates[i] = theirs[i - AHEAD]
@@ -388,13 +403,15 @@ def tile_list_merge_conflict_scores_kernel(
         scatter(0, 0, PIECE)
         scatter(0, PIECE, PIECE)
         quantize_wv(1, 1, values[0][:, :BANK].bitcast(BF16))
-        make_placed(0, slice(2 * PIECE, 3 * PIECE), wv_raw[1][:, :PIECE])
-        scatter_from(0, 2 * PIECE, PIECE, wv_raw[1][:, :PIECE])
+        nc.scalar.copy(wv_raw[1][:, S - ROW_TILES + 1 :], bg_turned[:, 1:ROW_TILES])
+        make_placed(0, slice(2 * PIECE, 3 * PIECE), wv_raw[1][:, BANK : BANK + PIECE])
+        scatter_from(0, 2 * PIECE, PIECE, wv_raw[1][:, BANK : BANK + PIECE])
+        make_placed(0, slice(3 * PIECE, 4 * PIECE), values[0][:, 2 * PIECE : 3 * PIECE])
+        scatter_from(0, 3 * PIECE, PIECE, values[0][:, 2 * PIECE : 3 * PIECE])
         quantize_wv(2, 1, sigs[0][:, BANK:].bitcast(BF16))
-        make_placed(0, slice(3 * PIECE, 4 * PIECE), wv_raw[2][:, :PIECE])
-        scatter_from(0, 3 * PIECE, PIECE, wv_raw[2][:, :PIECE])
+
         products(1, BANK)
-        theirs[0] = wv_raw[0]
+        theirs[0] = wv_raw[2]
         fetch(theirs[0][:], 0, idx4, 0, M)
         products(2, BANK)
 
@@ -435,6 +452,7 @@ def tile_list_merge_conflict_scores_kernel(
 
         def finish(c):
             if c >= EARLY:
+                quantize_z(0, chunk(c), first_pass[:, PACK * STARTS[c] : PACK * (STARTS[c] + WIDTHS[c])])
                 score_pass(0, c)
             quantize_z(1, chunk(c), stage[c % SLOTS][:, 0 : PACK * WIDTHS[c]])
             score_pass(1, c)
@@ -447,7 +465,7 @@ def tile_list_merge_conflict_scores_kernel(
             slots = [stage[c % SLOTS][:, s * w : (s + 1) * w] for s in range(3)]
             fetch(slots[0], last - 1, idx4, STARTS[c], w)
             if c == 0:
-                quantize_z(0, slice(0, M), first_pass)
+                quantize_z(0, slice(0, BANK), first_pass[:, : PACK * BANK])
                 for early in range(EARLY):
                     score_pass(0, early)
             fetch(slots[1], last, idx3, STARTS[c], w)

@@ -264,7 +264,10 @@ def tile_list_merge_conflict_scores_kernel(
                     nc.scalar.activation(sig[:, cols], pre[g][:, bank_cols], SIGMOID, bias=bias(i))
                     if count == PIECE:
                         nc.vector.tensor_tensor(value[:, cols], lin[g][:, bank_cols], gains[:, cols], MULT)
-                        nc.gpsimd.tensor_tensor(done[:, cols], sig[:, cols], value[:, cols], MULT)
+                        if g == 1:
+                            head = slice(0, PIECE)
+                            nc.vector.tensor_tensor(done[:, head], sig[:, head], value[:, head], MULT)
+                            nc.gpsimd.tensor_tensor(done[:, cols], sig[:, cols], value[:, cols], MULT)
                         continue
                     nc.scalar.copy(value[:, cols], lin[g][:, bank_cols])
                     if i < AHEAD:

from contextlib import ExitStack

import concourse.mybir as mybir
from concourse.masks import make_identity

K, H, N, T, S, T2, M = 1024, 1024, 512, 4096, 1024, 2048, 1024
FLOPS = 2 * (2 * K * H * S + H * N * M)

F32 = mybir.dt.float32
BF16 = mybir.dt.bfloat16
I32 = mybir.dt.int32
U32 = mybir.dt.uint32
U16 = mybir.dt.uint16
U8 = mybir.dt.uint8
FP8X4 = mybir.dt.float8_e4m3fn_x4
FP4X4 = mybir.dt.float4_e2m1fn_x4
MULT = mybir.AluOpType.mult
MAX = mybir.AluOpType.max
SUBTRACT = mybir.AluOpType.subtract
SIGMOID = mybir.ActivationFunctionType.Sigmoid
RELU = mybir.ActivationFunctionType.Relu

P = 128
PACK = 4
PASSES = 2
BANK = 512
ROW_TILES = H // P
TILES_PER_PASS = ROW_TILES // PASSES
WIDTHS = [256, 256, 256, 128, 128]
STARTS = [sum(WIDTHS[:c]) for c in range(len(WIDTHS))]
CHUNKS = len(WIDTHS)
N_TILES = N // P
LIST = 16
W4_HEAD = 3
AHEAD = 3
LAG = 2
EARLY = 2
SCORE_BANKS = 5
SLOTS = 3
ON_VECTOR = [(2, 1), (3, 0), (4, 1)]
PIECE = 256


def tile_list_merge_conflict_scores_kernel(
    tc, tab_words, tab_scales, offs, offs2, offs3, offs4, w4_words, w4_scales,
    bg, wv, wgs, page0, w8_words, w8_scales, out,
):
    nc = tc.nc
    with ExitStack() as ctx:
        lists = ctx.enter_context(tc.tile_pool(name="lists", bufs=1))
        keep = ctx.enter_context(tc.tile_pool(name="keep", bufs=1))
        ring = ctx.enter_context(tc.tile_pool(name="ring", bufs=2))
        shared = ctx.enter_context(tc.tile_pool(name="shared", bufs=1))
        psum = ctx.enter_context(tc.psum_pool(name="psum", bufs=1))

        def bank(number, shape, dtype, name):
            return psum.tile(shape, dtype, name="%s_bank%d" % (name, number), offset=2048 * number)


        def load_list(src, name):
            tile = lists.tile([P, S // LIST], U16, name=name)
            nc.sync.dma_start(tile[:], src)
            return tile

        def entries(tile, first, count):
            return tile[:, first // LIST : (first + count) // LIST]

        def zero_plane(plane):
            nc.vector.memset(plane[:].rearrange("p a c -> p (a c)").bitcast(I32), 0)

        def load_plane(queue, plane, scales):
            for q in range(4):
                queue.dma_start(
                    plane[:].bitcast(I32)[32 * q : 32 * q + 4, :, :],
                    scales.bitcast(I32)[:, 4 * q : 4 * q + 4, :].rearrange("a r c -> r a c"),
                )

        def move(engine, dst, src):
            if engine == "vector":
                nc.vector.tensor_copy(dst, src)
            else:
                nc.scalar.copy(dst, src)

        tab_plane = keep.tile([P, T], U8, align_bytes=64)
        nc.vector.memset(tab_plane[:].bitcast(I32), 0)
        head_cols = W4_HEAD * P
        w4_plane = [keep.tile([P, PASSES, w], U8, name="w4_plane%d" % w, align_bytes=64) for w in (head_cols, H - head_cols)]
        for plane in w4_plane:
            zero_plane(plane)

        def w4_scale(a, i):
            if i < W4_HEAD:
                return w4_plane[0][:, a, i * P : (i + 1) * P]
            return w4_plane[1][:, a, (i - W4_HEAD) * P : (i - W4_HEAD + 1) * P]

        bg_rows = keep.tile([P, P], F32)
        nc.gpsimd.memset(bg_rows[:], 0.0)
        nc.gpsimd.dma_start(bg_rows[0:ROW_TILES, :], bg.rearrange("(i p) -> i p", p=P))
        v_plane = [keep.tile([P, S], U8, name="v_plane%d" % a, align_bytes=64) for a in range(PASSES)]
        nc.vector.memset(v_plane[1][:].bitcast(I32), 0)
        w8_plane = keep.tile([P, PASSES, N], U8, align_bytes=64)
        zero_plane(w8_plane)
        ident_f32 = keep.tile([P, P], F32)
        make_identity(nc, ident_f32[:])
        ident_bf16 = keep.tile([P, P], BF16)
        nc.scalar.activation(ident_bf16[:], ident_f32[:], SIGMOID, scale=2000.0, bias=-1000.0)

        w4_src = w4_words.bitcast(I32).rearrange("a p c -> p a c")
        head_words = W4_HEAD * P // 2
        w4_head = keep.tile([P, PASSES, 4 * head_words], U8, align_bytes=64)
        w4_rest = keep.tile([P, PASSES, 2 * H - 4 * head_words], U8, align_bytes=64)

        def w4_codes(a, i):
            if i < W4_HEAD:
                return w4_head[:, a, 2 * P * i : 2 * P * (i + 1)]
            return w4_rest[:, a, 2 * P * (i - W4_HEAD) : 2 * P * (i - W4_HEAD + 1)]

        wv_raw = [
            shared.tile([P, PASSES * PACK * P], F32, name="wv_raw%d" % i, offset=32768 + 4096 * i, align_bytes=64)
            for i in range(ROW_TILES)
        ]
        pages = {}

        def raw_pass(i, a):
            return wv_raw[i][:, a * PACK * P : (a + 1) * PACK * P].rearrange("p (j c) -> p j c", j=PACK)

        def load_wv_pass(i, a):
            rows = wv[a * P * PACK : (a + 1) * P * PACK, i * P : (i + 1) * P]
            nc.sync.dma_start(raw_pass(i, a), rows.rearrange("(p j) c -> p j c", j=PACK))

        def load_wv(i):
            for a in range(PASSES):
                load_wv_pass(i, a)

        def load_page(i):
            page = ring.tile([P, T2], F32, name="page", bufs=5)
            nc.sync.dma_start(page[:], page0[i * P : (i + 1) * P, :])
            pages[i] = page

        tab = [shared.tile([P, T], I32, name="tab%d" % a, offset=16384 * a, align_bytes=64) for a in range(PASSES)]
        tab_src = [tab_words[a].rearrange("p t i -> p (t i)").bitcast(I32) for a in range(PASSES)]
        nc.sync.dma_start(tab[0][:, : T // 4], tab_src[0][:, : T // 4])
        rows = tab_scales.bitcast(I32).rearrange("a (q r) c -> r q a c", r=4)
        for r in range(4):
            nc.sync.dma_start(tab_plane[:].bitcast(I32)[r:P:16, :], rows[r])
        idx = load_list(offs, "idx")
        for cols in (slice(T // 4, 5 * T // 8), slice(5 * T // 8, T)):
            nc.sync.dma_start(tab[0][:, cols], tab_src[0][:, cols])
        nc.sync.dma_start(w4_head[:].bitcast(I32), w4_src[:, :, 0:head_words])
        load_plane(nc.sync, w4_plane[0], w4_scales[:, :, :head_cols])
        load_wv(0)
        for h in range(2):
            nc.sync.dma_start(tab[1][:, h * T // 2 : (h + 1) * T // 2], tab_src[1][:, h * T // 2 : (h + 1) * T // 2])
        idx2 = load_list(offs2, "idx2")
        idx3 = load_list(offs3, "idx3")
        idx4 = load_list(offs4, "idx4")
        gains = keep.tile([P, S], F32)
        nc.sync.dma_start(gains[:, :BANK], wgs[:, :BANK])
        load_page(0)
        nc.sync.dma_start(gains[:, BANK:], wgs[:, BANK:])
        load_wv(1)
        load_wv(2)
        load_page(1)
        nc.sync.dma_start(w4_rest[:].bitcast(I32), w4_src[:, :, head_words:])
        load_plane(nc.sync, w4_plane[1], w4_scales[:, :, head_cols:])
        load_wv(3)
        load_wv(4)
        load_page(2)
        load_wv(5)
        load_page(3)
        load_wv(6)
        load_wv(7)
        load_page(4)
        w8_codes = keep.tile([P, PASSES, N], I32, align_bytes=64)
        nc.sync.dma_start(w8_codes[:], w8_words.rearrange("a p c i -> p a (c i)").bitcast(I32))
        load_plane(nc.sync, w8_plane, w8_scales)

        bg_turned = bank(7, [P, P], F32, "bias")
        nc.tensor.transpose(bg_turned[:], bg_rows[:], ident_f32[:])
        bias_first = keep.tile([P, 1], F32)
        nc.scalar.copy(bias_first[:], bg_turned[:, 0:1])

        def bias(i):
            if i == 0:
                return bias_first[:]
            return wv_raw[1][:, S - ROW_TILES + i : S - ROW_TILES + i + 1]

        v_codes = [keep.tile([P, S], U32, name="v_codes%d" % a, align_bytes=64) for a in range(PASSES)]
        nc.vector.tensor_copy(v_plane[0][:], tab_plane[:].indirect(idx[:]))
        nc.gpsimd.dma_start(v_plane[1][:].bitcast(I32)[0:100, :], v_plane[0][:].bitcast(I32)[16:116, :])
        nc.vector.tensor_copy(v_codes[0][:], tab[0][:].bitcast(U32).indirect(idx[:]))

        def gather_second_pass():
            for h in range(S // BANK):
                nc.vector.tensor_copy(
                    v_codes[1][:, h * BANK : (h + 1) * BANK],
                    tab[1][:].bitcast(U32).indirect(entries(idx, h * BANK, BANK)),
                )

        width = PASSES * P
        wv_codes = keep.tile([P, ROW_TILES * width], U32, align_bytes=64)
        wv_plane = keep.tile([P, ROW_TILES * width], U8, align_bytes=64)

        def quantize_wv(first, count, grouped):
            for e in range(count):
                for a in range(PASSES):
                    start = (e * PASSES + a) * P * PACK
                    nc.scalar.copy(
                        grouped[:, start : start + P * PACK].rearrange("p (c e j) -> p c j e", e=4, j=PACK),
                        raw_pass(first + e, a).rearrange("p j (c e) -> p c j e", e=4),
                    )
            cols = slice(first * width, (first + count) * width)
            nc.vector.quantize_mx(
                out=wv_codes[:, cols].bitcast(FP8X4), scales=wv_plane[:, cols], in_=grouped[:, 0 : count * width * PACK]
            )

        sigs, gates, values, placed, theirs = {}, {}, {}, {}, {}

        def make_gate(i, cols):
            nc.gpsimd.tensor_tensor(gates[i][:, cols], sigs[i][:, cols], gains[:, cols], MULT)

        def make_placed(i, cols, dst):
            nc.gpsimd.tensor_tensor(dst, gates[i][:, cols], values[i][:, cols], MULT)

        def products(i, piece):
            sigs[i] = sig = ring.tile([P, S], F32, name="sig", align_bytes=64)
            value = ring.tile([P, S], F32, name="value", bufs=3, align_bytes=64)
            if i < AHEAD:
                gates[i] = ring.tile([P, S], F32, name="gate", bufs=1, align_bytes=64)
                placed[i] = done = ring.tile([P, S], F32, name="placed", align_bytes=64)
            values[i] = value
            spans = [(0, PIECE), (PIECE, PIECE), (BANK, BANK)] if i == 0 else [(0, BANK), (BANK, BANK)]
            numbers = [0, 4, 2] if i == 0 else [0, 2]
            pre = [bank(n + i % 2, [P, count], F32, "pre") for n, (first, count) in zip(numbers, spans)]
            lin = [bank(n + (i + 1) % 2, [P, count], F32, "lin") for n, (first, count) in zip(numbers, spans)]

            def one_pass(acc, codes, plane, a, first, count, step):
                for local in range(0, count, step):
                    cols = slice(first + local, first + local + step)
                    nc.tensor.matmul_mx(
                        out=acc[:, local : local + step],
                        lhsT=codes,
                        lhsT_scale=plane,
                        rhs=v_codes[a][:, cols].bitcast(FP8X4),
                        rhs_scale=v_plane[a][:, cols],
                        start=(a == 0 and local == 0),
                        stop=(a == PASSES - 1 and local + step == count),
                    )

            def both(a, g):
                first, count = spans[g]
                cols = slice(i * width + a * P, i * width + (a + 1) * P)
                one_pass(pre[g], w4_codes(a, i).bitcast(FP4X4), w4_scale(a, i), a, first, count, BANK if count == BANK else P)
                one_pass(lin[g], wv_codes[:, cols].bitcast(FP8X4), wv_plane[:, cols], a, first, count, count)

            order = [(a, g) for g in range(len(spans)) for a in range(PASSES)]
            if i == 0:
                order = [(a, g) for a in range(PASSES) for g in range(len(spans))]
            for a, g in order:
                both(a, g)
            for g, (start, count) in enumerate(spans):
                for local in range(0, count, piece):
                    cols, bank_cols = slice(start + local, start + local + piece), slice(local, local + piece)
                    nc.scalar.activation(sig[:, cols], pre[g][:, bank_cols], SIGMOID, bias=bias(i))
                    if count == PIECE:
                        nc.vector.tensor_tensor(value[:, cols], lin[g][:, bank_cols], gains[:, cols], MULT)
                        if g == 1:
                            head = slice(0, PIECE)
                            nc.vector.tensor_tensor(done[:, head], sig[:, head], value[:, head], MULT)
                            nc.gpsimd.tensor_tensor(done[:, cols], sig[:, cols], value[:, cols], MULT)
                        continue
                    nc.scalar.copy(value[:, cols], lin[g][:, bank_cols])
                    if i < AHEAD:
                        make_gate(i, cols)
                    if 0 < i < AHEAD:
                        make_placed(i, cols, done[:, cols])

        def combine(i):
            gates[i] = theirs[i - AHEAD]
            placed[i] = ring.tile([P, S], F32, name="placed", align_bytes=64)
            for first in range(0, S, BANK):
                cols = slice(first, first + BANK)
                make_gate(i, cols)
                make_placed(i, cols, placed[i][:, cols])

        def scatter_from(i, first, count, src):
            nc.vector.tensor_copy(pages[i][:].indirect(entries(idx2, first, count)), src)

        def scatter(i, first, count):
            scatter_from(i, first, count, placed[i][:, first : first + count])

        def fetch(dst, i, lst, first, count):
            nc.vector.tensor_copy(dst, pages[i][:].indirect(entries(lst, first, count)))

        rows0_tile = shared.tile([P, M * PACK], BF16, offset=0, align_bytes=64)
        rows0 = rows0_tile[:].rearrange("p (b u q e) -> p b u q e", u=2, q=P, e=2)
        first_pass_tile = shared.tile([P, M * PACK], BF16, offset=8192, align_bytes=64)
        first_pass = first_pass_tile[:]
        rows1_tile = keep.tile([P, M * PACK], BF16, align_bytes=64)
        rows1 = rows1_tile[:].rearrange("p (b u q e) -> p b u q e", u=2, q=P, e=2)

        def rows_of(c):
            return rows1[:, STARTS[c] // P : (STARTS[c] + WIDTHS[c]) // P]


        excesses = {}

        def difference(i, dst):
            nc.vector.tensor_tensor(dst[:], pages[i][:].indirect(idx3[:]), theirs[i][:], SUBTRACT)
            if i == TILES_PER_PASS:
                excess = rows0_tile[:].bitcast(F32)[:, 0:M]
            else:
                excess = ring.tile([P, M], F32, name="excess", align_bytes=64)
            excesses[i] = excess
            a, slot = divmod(i, TILES_PER_PASS)
            q_cols = slice(slot * P // PACK, (slot + 1) * P // PACK)
            for h in range(M // BANK):
                cols = slice(h * BANK, (h + 1) * BANK)
                nc.scalar.activation(excess[:, cols], dst[:, cols], RELU)
            for h in range(M // BANK):
                turned = bank({5: 0}.get(i, 4) + h, [P, BANK // P, P], F32, "sum")
                for term, src in enumerate((theirs[i], excess)):
                    for b in range(BANK // P):
                        nc.tensor.matmul(
                            turned[:, b, :],
                            src[:, h * BANK + b * P : h * BANK + (b + 1) * P],
                            ident_f32[:],
                            start=(term == 0 and b == 0),
                            stop=(term == 1 and b == BANK // P - 1),
                            is_transpose=True,
                        )
                pairs = turned[:].rearrange("p b (q u e) -> p b u q e", u=2, e=2)
                nc.scalar.copy((rows0, rows1)[a][:, h * BANK // P : (h + 1) * BANK // P, :, q_cols, :], pairs)

        def as_words(rows):
            return rows.rearrange("p b u q e -> p b u (q e)").bitcast(F32)

        def turn_first(c, best, engine):
            blocks = WIDTHS[c] // P
            turned = bank(5, [P, blocks, 2, P], BF16, "first")
            for e in range(2):
                for b in range(blocks):
                    nc.tensor.transpose(turned[:, b, e, :], best[:, e, b * P : (b + 1) * P], ident_bf16[:])
            move(
                engine,
                as_words(rows_of(c))[:, :, :, P // 2 :],
                turned[:].rearrange("p b e r -> p b (e r)").bitcast(F32).rearrange("p b (q u) -> p b u q", u=2),
            )

        def turn_second(number, words, blocks, grouped, engine):
            turned = bank(number, [P, blocks, 2, P], F32, "second")
            for b in range(blocks):
                for u in range(2):
                    nc.tensor.transpose(turned[:, b, u, :], words[:, b, u, :], ident_f32[:])
            move(
                engine,
                grouped.bitcast(F32).rearrange("p (b m u) -> p b m u", b=blocks, u=2),
                turned[:].rearrange("p b u m -> p b m u"),
            )

        z_codes = {1: keep.tile([P, M], U32, name="z_codes", align_bytes=64)}
        z_plane = [keep.tile([P, M], U8, name="z_plane%d" % a, align_bytes=64) for a in range(PASSES)]

        def chunk(c):
            return slice(STARTS[c], STARTS[c] + WIDTHS[c])

        def quantize_z(a, cols, grouped):
            nc.vector.quantize_mx(out=z_codes[a][:, cols].bitcast(FP8X4), scales=z_plane[a][:, cols], in_=grouped)

        sums = {}

        def banks(c):
            per_bank = 2 if c == CHUNKS - 1 else BANK // WIDTHS[c]
            return [range(t, t + per_bank) for t in range(0, N_TILES, per_bank)]

        def score_pass(a, c):
            for g, tiles in enumerate(banks(c)):
                if a == 0:
                    number = (N_TILES * STARTS[c] // BANK + g) % SCORE_BANKS
                    sums[c, g] = bank(number, [P, len(tiles), WIDTHS[c]], F32, "score")
                for e, t in enumerate(tiles):
                    nc.tensor.matmul_mx(
                        out=sums[c, g][:, e, :],
                        lhsT=w8_codes[:, a, t * P : (t + 1) * P].bitcast(FP8X4),
                        lhsT_scale=w8_plane[:, a, t * P : (t + 1) * P],
                        rhs=z_codes[a][:, chunk(c)].bitcast(FP8X4),
                        rhs_scale=z_plane[a][:, chunk(c)],
                        start=(a == 0 and e == 0),
                        stop=(a == PASSES - 1 and e == len(tiles) - 1),
                    )

        out_tiles = out.rearrange("(t p) m -> p t m", p=P)
        staged = shared.tile([P, N_TILES * M], F32, offset=16384, align_bytes=64)

        def store_scores(c):
            for g, tiles in enumerate(banks(c)):
                first = N_TILES * STARTS[c] + tiles.start * WIDTHS[c]
                piece = staged[:, first : first + len(tiles) * WIDTHS[c]].rearrange("p (e m) -> p e m", e=len(tiles))
                move("vector" if (c, g) in ON_VECTOR else "scalar", piece, sums[c, g][:])
                nc.sync.dma_start(out_tiles[:, tiles.start : tiles.stop, chunk(c)], piece)

        grouped0 = keep.tile([P, width * PACK], BF16, align_bytes=64)
        quantize_wv(0, 1, grouped0[:])
        gather_second_pass()
        products(0, PIECE)
        scatter(0, 0, PIECE)
        scatter(0, PIECE, PIECE)
        quantize_wv(1, 1, values[0][:, :BANK].bitcast(BF16))
        nc.scalar.copy(wv_raw[1][:, S - ROW_TILES + 1 :], bg_turned[:, 1:ROW_TILES])
        make_placed(0, slice(2 * PIECE, 3 * PIECE), wv_raw[1][:, BANK : BANK + PIECE])
        scatter_from(0, 2 * PIECE, PIECE, wv_raw[1][:, BANK : BANK + PIECE])
        make_placed(0, slice(3 * PIECE, 4 * PIECE), values[0][:, 2 * PIECE : 3 * PIECE])
        scatter_from(0, 3 * PIECE, PIECE, values[0][:, 2 * PIECE : 3 * PIECE])
        quantize_wv(2, 1, sigs[0][:, BANK:].bitcast(BF16))

        products(1, BANK)
        theirs[0] = wv_raw[2]
        fetch(theirs[0][:], 0, idx4, 0, M)
        products(2, BANK)

        last = ROW_TILES - 1
        for i in range(1, last - 1):
            if i == 1:
                for first in range(0, S, BANK):
                    scatter(i, first, BANK)
            else:
                difference(i - LAG, gates[i])
                combine(i + 1)
                if i + AHEAD < ROW_TILES:
                    load_page(i + AHEAD)
                scatter(i, 0, S)
            if i + AHEAD < ROW_TILES:
                quantize_wv(AHEAD if i == 1 else i + AHEAD, 2 if i == 1 else 1, values[i][:].bitcast(BF16))
                theirs[i] = wv_raw[i + AHEAD]
                fetch(theirs[i][:], i, idx4, 0, M)
            products(i + LAG, BANK)
        words = as_words(rows0)
        for b in range(0, M // P, 2):
            turn_second(b // 2, words[:, b : b + 2], 2, first_pass[:, PACK * P * b : PACK * P * (b + 2)], "scalar")

        difference(last - 3, gates[last - 1])
        combine(last)
        theirs[last - 2] = values[last - 1]
        fetch(theirs[last - 2][:], last - 2, idx4, 0, M)
        scatter(last - 1, 0, S)
        difference(last - 2, gates[last])
        ours = values[last][:, :BANK].bitcast(BF16)
        fetch(ours, last - 1, idx3, 0, M)
        scatter(last, 0, S)

        slot_cols = PACK * max(WIDTHS)
        spent = ring.tile([P, 2 * slot_cols], BF16, name="placed", align_bytes=64)
        stage = [values[last][:, BANK:].bitcast(BF16), spent[:, :slot_cols], spent[:, slot_cols:]]
        z_codes[0] = ring.tile([P, M], U32, name="placed", align_bytes=64)

        def finish(c):
            if c >= EARLY:
                quantize_z(0, chunk(c), first_pass[:, PACK * STARTS[c] : PACK * (STARTS[c] + WIDTHS[c])])
                score_pass(0, c)
            quantize_z(1, chunk(c), stage[c % SLOTS][:, 0 : PACK * WIDTHS[c]])
            score_pass(1, c)
            store_scores(c)

        for c in range(CHUNKS):
            w = WIDTHS[c]
            if c >= SLOTS:
                finish(c - SLOTS)
            slots = [stage[c % SLOTS][:, s * w : (s + 1) * w] for s in range(3)]
            fetch(slots[0], last - 1, idx4, STARTS[c], w)
            if c == 0:
                quantize_z(0, slice(0, BANK), first_pass[:, : PACK * BANK])
                for early in range(EARLY):
                    score_pass(0, early)
            fetch(slots[1], last, idx3, STARTS[c], w)
            fetch(slots[2], last, idx4, STARTS[c], w)
            best = ring.tile([P, 2, w], BF16, name="best")
            nc.vector.tensor_tensor(best[:, 0, :], ours[:, chunk(c)], slots[0], MAX)
            nc.vector.tensor_tensor(best[:, 1, :], slots[1], slots[2], MAX)
            engine = "vector" if c == CHUNKS - 1 else "scalar"
            turn_first(c, best, engine)
            turn_second(6 + c % 2, as_words(rows_of(c)), w // P, stage[c % SLOTS][:, 0 : PACK * w], engine)
        for c in range(CHUNKS - SLOTS, CHUNKS):
            finish(c)
